import numpy as np, ml_dtypes
CORES = [3,11,19,27,35,43,51,59]
N = 8
import mx_ref
BF = ml_dtypes.bfloat16
def gentries(a):
    return np.ascontiguousarray(a.reshape(8, 16, -1).transpose(0, 2, 1)).reshape(8, -1)
def gtable(e):
    e = np.asarray(e); return np.ascontiguousarray(e.reshape(8, -1, 16).transpose(0, 2, 1)).reshape(128, -1).astype(np.int32)
def gcols(t, e):
    v = np.concatenate([t.reshape(8, 16, -1, 4), np.zeros((8, 16, 1, 4), BF)], axis=2)
    return np.ascontiguousarray(np.stack([v[g][:, e[g]] for g in range(8)])).reshape(128, -1)
def tile(rs):
    return np.stack(rs, axis=2).reshape(128, -1).astype(BF)
def pick(q, e):
    c = np.concatenate([q[0].reshape(128, -1, 4), np.zeros((128, 1, 4), np.uint8)], axis=1); s = np.concatenate([q[1], np.ones((16, 1), np.uint8)], axis=1)
    return (np.ascontiguousarray(c[:, e].reshape(128, -1)), np.ascontiguousarray(s[:, e]))
def join(*qs):
    return (np.concatenate([q[0] for q in qs], axis=1), np.concatenate([q[1] for q in qs], axis=1))
def put(q, e, v):
    c, s = q[0].reshape(128, -1, 4).copy(), q[1].copy(); c[:, e] = v[0].reshape(128, -1, 4); s[:, e] = v[1]
    return (c.reshape(128, -1), s)
def pk(c, s):
    return (np.ascontiguousarray(c), mx_ref.live(s))
def emit(q):
    return q[0], q[1]
def packed(v, rng):
    q = [mx_ref.quantize(np.ascontiguousarray(v[r])) for r in range(N)]
    return np.stack([a for a, b in q]), np.stack([mx_ref.plane(b, rng) for a, b in q])
def values_of_codes():
    e, c = np.zeros((128, 128, 4), np.float32), np.zeros((128, 2, 4), np.uint8)
    e[np.arange(128), np.arange(128), 0] = 1
    c[:127, :, 0] = np.arange(256).reshape(2, 128).T[:127]
    return mx_ref.matmul(mx_ref.quantize(e.reshape(128, 512).astype(BF)), (c.reshape(128, 8), np.full((16, 2), 127, np.uint8))).T.reshape(-1).astype(np.float64)
CODE_VALUE, SCALE_VALUE = values_of_codes(), 2.0 ** (np.arange(256) - 127.0)
def decode(q):
    return (CODE_VALUE[q[0]].reshape(16, 8, -1, 4) * SCALE_VALUE[q[1]][:, None, :, None] + 0.0).reshape(128, -1).astype(np.float32)
def f(rng, *shape):
    return mx_ref.flush((rng.standard_normal(shape, dtype=np.float32) * np.exp2(rng.integers(-2, 3, shape[:-1] + (1,)))).astype(BF))
def wide(rng, *shape, cols=0):
    v = rng.standard_normal(shape, dtype=np.float32) * np.exp2(rng.integers(-12, 13, shape)).astype(np.float32)
    if cols: v *= np.repeat(np.exp2(rng.integers(-cols, cols + 1, shape[:-2] + (1, shape[-1] // 4))) * (rng.random(shape[:-2] + (1, shape[-1] // 4)) > 0.0625), 4, axis=-1).astype(np.float32)
    return mx_ref.flush(v.astype(BF))
C = 320
STEP = [1, 2, 4]
def numbers_of(rng):
    return {"x": np.array(f(rng, N, 128, 4 * C)), "u": np.array(f(rng, N, 128, 512)), "v": np.array(f(rng, N, 128, 512))}
def stored(h, t):
    return {"hl": np.stack([gtable(h[r]) for r in range(N)]), "tl": np.stack([gtable(t[r]) for r in range(N)])}
def lists(rng):
    e = np.tile(np.arange(C), (N, 8, 1))
    return stored(rng.permuted(e, axis=2), rng.permuted(e, axis=2))
def layers(rng, still=()):
    w = np.array(f(rng, N, 128, 2048)).reshape(N, 8, 16, 4, 8, 16, 4)
    for i in still:
        w[:, :, i] = 0
        w[:, :, :, :, :, i] = 0
    return w
def weights(rng, w):
    c, s = packed(np.ascontiguousarray(w).reshape(N, 128, 2048), rng)
    return {"wc": c, "ws": s}
def setup_inputs(rng):
    return {**numbers_of(rng), **lists(rng), **weights(rng, layers(rng))}
def setup_inputs_ties(rng):
    d = numbers_of(rng)
    o = rng.permutation(N)
    k = rng.integers(0, 4, (N, 2, 8, C))
    k[o[1]] += 1
    for g in rng.permutation(8)[:4]: k[o[2], :, g] = 1
    x = d["x"].reshape(N, 8, 16, C, 4)
    u = d["u"].reshape(N, 128, 128, 4)
    for i in range(2):
        x[:, :, i] = 0
        x[:, :, i, :, 0] = k[:, i].astype(np.float32).astype(BF)
        u[:, :, i::16] = 0
        for r in range(N):
            for h in range(i, 128, 16): u[r, h, h, 0] = 0.0 if r == o[0] else -1.0 if r == o[1] else 1.0
    a = np.exp2(rng.integers(-3, 4, (8, 1)).astype(np.float32))
    x[:, :, 8:] = 0
    x[:, :, 8, :, 0] = (-1.125 * a).astype(BF)
    x[:, :, 10, :, 0] = (-0.0703125 * a).astype(BF)
    w = layers(rng, [0, 1])
    w[:, :, :, :, :, 8:] = 0
    for g in range(8):
        w[:, g, 8, 0, g, 8, 0] = -28.0
        for b in range(4): w[:, g, 10, b, g, 9, 0] = -2.0 ** (b - 5)
    return {"x": x.reshape(N, 128, 4 * C), "u": u.reshape(N, 128, 512), "v": d["v"], **lists(rng), **weights(rng, w)}
def setup_inputs_near(rng):
    d = numbers_of(rng)
    x = d["x"].astype(np.float32).reshape(N, 8, 16, C, 4)
    x[:, :, 0] = 0
    x[:, :, 8:] = 0
    u = d["u"].reshape(N, 128, 128, 4)
    for i in range(2): u[:, :, i::16] = 0
    w = layers(rng, [0, 8, 9, 10, 11, 12, 13, 14, 15])
    o = rng.permutation(N) % 4
    for r in range(N):
        c = rng.choice([-1.0, 1.0], (8, 1))
        k = 1.0 if o[r] == 0 else 2.0 ** -30
        if o[r] < 2:
            x[r, :, 0, :, 0] = c
            x[r, :, 11, :, 0] = 2.0 ** -10
        x[r, :, 13, :, 0] = rng.integers(0, 2, (8, C)) * (2.0 ** -20 if o[r] < 2 else 2.0 ** -30)
        x[r, :, 15, :, 0] = 2.0 ** -20 if o[r] < 2 else 2.0 ** -29
        for g in range(8):
            w[r, g, 13, 0, g, 12, 0] = 2.0 ** -18 if o[r] < 2 else 2.0 ** -8
            if o[r] < 2: w[r, g, 14, 0, g, 12, 0] = 2.0 ** -6
            w[r, g, 15, 0, g, 15, 0] = 2.0 ** -5 if o[r] < 2 else 16.0
        for i in range(2):
            s = rng.integers(0, 16, (8, C))
            digits = ((s[:, :, None] >> np.arange(4)) & 1) * np.exp2(np.arange(4) - 23.0)
            if o[r] < 2: x[r, :, 8 + i] = digits
            elif o[r] == 2: x[r, :, 8 + i] = digits * rng.choice([-1.0, 1.0], (8, C, 1))
            else:
                x[r, :, 8 + 2 * i, :, 0] = np.where(s < 8, 1.25, 0.0) * 2.0 ** -30 * c
                x[r, :, 9 + 2 * i, :, 0] = np.where(s < 8, 0.0, 1.125) * 2.0 ** -30 * c
                for g in rng.permutation(8)[:4]:
                    e = rng.choice([-1.0, 1.0], C) * 2.0 ** -30
                    x[r, g, 8 + 2 * i, :, 0] = 1.25 * e
                    x[r, g, 9 + 2 * i, :, 0] = -1.125 * e
            for p in range(0, 128, 16):
                u[r, p, p + i, 0] = k if o[r] < 2 else 1.0
                u[r, p + 12, p + i, 0] = k
                if o[r] < 2: u[r, p + 11, p + i, 0] = k
                if o[r] < 3: u[r, p + 8 + i, p + i] = k
                else:
                    u[r, p + 8 + 2 * i, p + i, 0] = k
                    u[r, p + 9 + 2 * i, p + i, 0] = 1.125 * k
        at = [0, C - 1, int(rng.integers(C)), int(rng.integers(C))]
        for g, j in zip(rng.permutation(8)[:4], at): x[r, g, 0, j, 0] = 2.0 ** 29 * rng.choice([-1.0, 1.0])
    return {"x": x.reshape(N, 128, 4 * C).astype(BF), "u": u.reshape(N, 128, 512), "v": d["v"], **lists(rng), **weights(rng, w)}
def setup_inputs_odd(rng):
    d = numbers_of(rng)
    x = (1.0 + (2 * rng.integers(0, 64, (N, 16, 8, C, 4)) + 1) * 2.0 ** -7) * np.exp2(-rng.integers(0, 7, (N, 16, 8, C, 4)).astype(np.float64)) * rng.choice([-1.0, 1.0], (N, 16, 8, C, 4))
    x[:, :, 0, :, 0] = 1.96875 * 2.0 ** 8 * rng.choice([-1.0, 1.0], (N, 16, 1))
    u = d["u"].reshape(N, 128, 128, 4)
    for i in range(2):
        x[:, ::2, 1 + i, :, 0] = (8 + rng.integers(0, 2, (N, 8, C))) * 2.0 ** -8
        u[:, :, i::16] = 0
        for h in range(i, 128, 16): u[:, h + 1, h, 0] = 1.0
    return {"x": x.astype(np.float32).reshape(N, 128, 4 * C).astype(BF), "u": u.reshape(N, 128, 512), "v": d["v"], **lists(rng), **weights(rng, layers(rng, [0, 8]))}
def setup_inputs_ends(rng):
    d = numbers_of(rng)
    x = np.zeros((N, 8, 16, C, 4))
    u = d["u"].astype(np.float32).reshape(N, 128, 128, 4)
    v = d["v"].astype(np.float32)
    w = np.zeros((N, 128, 4, 128, 4), np.float32)
    hh, tt = np.zeros((N, 8, C), np.int64), np.zeros((N, 8, C), np.int64)
    o, e = rng.permutation(N) % 4, rng.permutation(N) % 4
    i, a = np.arange(128), np.arange(C)
    for r in range(N):
        low = -(0.8 + 0.08 * rng.random((8, 16, C, 4))) * 2.0 ** 30
        low[:, 15] = -2.0 ** 30
        tiny = -(1.0 + 0.125 * rng.integers(0, 8, (8, 16, C, 4))) * 2.0 ** -30
        if o[r] == 0: x[r] = low
        if o[r] == 1: x[r] = np.where((rng.random(C) < 0.5)[:, None], -low, low)
        if o[r] == 2: x[r] = tiny
        if o[r] == 3: x[r] = d["x"][r].astype(np.float32).reshape(8, 16, C, 4)[:, :, :1]
        x[r, 0] = tiny[0] * 2.0 ** 20 if o[r] < 2 else tiny[0] if o[r] == 2 else -2.0 ** -30
        for k in range(2):
            h = rng.permutation(8)
            c = np.where(h < 2, 0.0, h % 2 * 2.0 - 1.0)[None, :, None]
            if o[r] < 2: u[r, :, k::16] = c * (0.9 + 0.1 * rng.random((128, 8, 4))) * 2.0 ** 30
            if o[r] == 2: u[r, :, k::16] = c * (1.0 + 0.125 * rng.integers(0, 8, (128, 8, 4))) * 2.0 ** -30
            if o[r] == 3: u[r, :, k::16] *= np.abs(c).astype(np.float32)
        if o[r] < 2: v[r] = rng.choice([-1.0, 1.0], (128, 512)) * (0.9 + 0.1 * rng.random((128, 512))) * 2.0 ** 30
        else: v[r] = rng.choice([-1.0, 1.0], (128, 512)) * (1.0 + 0.125 * rng.integers(0, 8, (128, 512))) * 2.0 ** -30
        k = np.array([0.25, 0.5, 1.0])[rng.permutation(8) % 3] * rng.choice([-1.0, 1.0], 8)
        if o[r] == 2: k[:] = 0.0
        k[0] = 2.0 ** 8 if o[r] > 1 else 2.0 ** -8
        for b in range(4): w[r, i, b, i, b] = np.where((i >= 16) & (i % 16 == 15), 0.0, k[i // 16])
        hh[r] = C - 1 - a if e[r] == 1 else a
        if e[r] == 3: hh[r] = rng.permuted(np.tile(a, (8, 1)), axis=1)
        tt[r] = hh[r] if e[r] < 2 else np.roll(a, 1) if e[r] == 2 else hh[r] ^ 1
    return {"x": x.astype(np.float32).reshape(N, 128, 4 * C).astype(BF), "u": u.reshape(N, 128, 512).astype(BF), "v": v.astype(BF), **stored(hh, tt), **weights(rng, w.astype(BF))}
def setup_inputs_spread(rng):
    d = setup_inputs(rng)
    d["x"] = wide(rng, N, 128, 4 * C, cols=6)
    return d
def check_inputs(d):
    b = []
    for k in ("x", "u", "v"):
        a = np.abs(d[k].astype(np.float32))
        if not (np.isfinite(a).all() and ((a == 0) | (a >= 2.0 ** -30) & (a <= 2.0 ** 30)).all()): b.append("a value of " + k)
    for k in ("hl", "tl"):
        for r in range(N):
            if not (np.sort(gentries(d[k][r]), axis=1) == np.arange(C)).all(): b.append(k + ": every number once in a group")
    none, least, most = [emit(mx_ref.quantize(np.full((128, 16), k, np.float32).astype(BF)))[1][0, 0] for k in (0.0, 2.0 ** -8, 2.0 ** 8)]
    for r in range(N):
        if ((d["wc"][r] == 0x7F) | (d["wc"][r] == 0xFF)).any(): b.append("wc: a code that is no number")
        s = mx_ref.live(d["ws"][r])
        if ((s != none) & ((s < least) | (s > most))).any(): b.append("ws: a scale out of range")
    return b
def ordered(s, a):
    e = np.sort(np.argsort(a, axis=1).reshape(8, -1, 2), axis=2)
    k = np.take_along_axis(s, e.reshape(8, -1), axis=1).reshape(e.shape)
    return np.where((k[:, :, 1] > k[:, :, 0])[:, :, None], e[:, :, ::-1], e).reshape(8, -1)
def transition(s, h, t):
    m = np.zeros((8, C), np.int64)
    np.put_along_axis(m, ordered(s, h), ordered(s, t), axis=1)
    return m
def behind(a, e):
    return np.take_along_axis(a, e, axis=1)
def reference(x, u, v, hl, tl, wc, ws):
    qu = [mx_ref.quantize(u[r]) for r in range(N)]
    lay = [pk(wc[r], ws[r]) for r in range(N)]
    now = [x[r] for r in range(N)]
    head, tail = [gentries(hl[r]) for r in range(N)], [gentries(tl[r]) for r in range(N)]
    for step in STEP:
        way, made = [], []
        for r in range(N):
            s = mx_ref.matmul(qu[r], mx_ref.quantize(now[r])) + np.float32(0.0)
            m0, m1 = transition(s[0::16], head[r], tail[r]), transition(s[1::16], head[r], tail[r])
            way.append(behind(m1, m0))
            z = mx_ref.quantize(((gcols(now[r], m0).astype(np.float32) + gcols(now[r], way[r]).astype(np.float32)) * np.float32(0.5)).astype(BF))
            made.append(mx_ref.quantize(tile([mx_ref.matmul(pick(lay[r], np.arange(128 * b, 128 * b + 128)), z) * np.float32(0.03125) for b in range(4)])))
        for r in range(N):
            p = r ^ step
            far = gcols(decode(made[p]).astype(BF), behind(way[r], way[p]))
            now[r] = (now[r].astype(np.float32) + far.astype(np.float32)).astype(BF)
            head[r], tail[r] = tail[r], behind(head[r], way[p])
    y, tp = np.zeros((N, 128, C), np.float32), np.zeros((N, 8, C), np.float32)
    oc, osc = np.zeros((N, 128, 4 * C), np.uint8), np.zeros((N, 16, C), np.uint8)
    for r in range(N):
        q = mx_ref.quantize(now[r])
        y[r] = mx_ref.matmul(mx_ref.quantize(v[r]), q)
        tp[r] = tail[r]
        oc[r], osc[r] = emit(q)
    return {"y": y, "tp": tp, "oc": oc, "osc": osc}

@@ -1,0 +1,421 @@
+from concourse.mybir import dt, AluOpType, ActivationFunctionType
+
+A = AluOpType
+AF = ActivationFunctionType
+C = 320
+HC = 160
+STEP = [1, 2, 4]
+CODE = "float8_e4m3fn_x4"
+
+SCRATCH = {
+    "cio": ("sbuf", [128, 320], "float32"), "dec": ("sbuf", [128, 320], "float32"),
+    "him": ("sbuf", [128, 320], "int32"), "hia": ("sbuf", [128, 320], "int32"), "mk": ("sbuf", [128, 320], "float32"),
+    "hold": ("sbuf", [128, 320], "float32"), "holdb": ("sbuf", [128, 320], "bfloat16"), "alt": ("sbuf", [128, 320], "bfloat16"),
+    "pmi": ("sbuf", [128, 2], "int32"), "pma": ("sbuf", [128, 2], "int32"), "sub": ("sbuf", [128, 1], "float32"),
+    "cp": ("sbuf", [128, 1], "float32"), "cp2": ("sbuf", [128, 1], "float32"), "ciw": ("sbuf", [128, 320], "float32"),
+    "uoi": ("sbuf", [128, 16], "int32"), "uof": ("sbuf", [128, 16], "uint16"),
+    "one": ("sbuf", [128, 512], "bfloat16"), "et": ("sbuf", [128, 2048], "bfloat16"),
+    "qe": ("sbuf", [128, 512], CODE), "se": ("sbuf", [128, 512], "uint8"),
+    "ut": ("sbuf", [128, 512], "bfloat16"), "vt": ("sbuf", [128, 512], "bfloat16"),
+    "qu": ("sbuf", [128, 128], CODE), "su": ("sbuf", [128, 128], "uint8"),
+    "qu2": ("sbuf", [128, 256], CODE), "su2": ("sbuf", [128, 256], "uint8"),
+    "qv": ("sbuf", [128, 128], CODE), "sv": ("sbuf", [128, 128], "uint8"),
+    "qw": ("sbuf", [128, 512], CODE), "sw": ("sbuf", [128, 512], "uint8"),
+    "hlt": ("sbuf", [128, 40], "int32"), "hb": ("sbuf", [128, 40], "int32"), "hv": ("sbuf", [128, 40], "int32"),
+    "hb2": ("sbuf", [128, 40], "int32"), "enci": ("sbuf", [128, 40], "int32"),
+    "xp": ("sbuf", [128, 1280], "bfloat16"), "y32": ("sbuf", [128, 1280], "float32"), "zt": ("sbuf", [128, 1280], "bfloat16"),
+    "ht": ("sbuf", [128, 1280], "bfloat16"), "dd": ("sbuf", [128, 1280], "bfloat16"),
+    "qz": ("sbuf", [128, 320], CODE), "sz": ("sbuf", [128, 320], "uint8"),
+    "qx": ("sbuf", [128, 320], CODE), "sx": ("sbuf", [128, 320], "uint8"),
+    "qo": ("sbuf", [128, 320], CODE), "so": ("sbuf", [128, 320], "uint8"),
+    "yo": ("sbuf", [128, 320], "float32"), "tpr": ("sbuf", [128, 320], "float32"),
+    "ps": ("psum", [128, 4096], "float32"),
+    "mt": ("sbuf", [128, 40], "float32"), "mf": ("sbuf", [128, 40], "float32"), "er": ("sbuf", [128, 640], "float32"),
+    "g2": ("sbuf", [128, 40], "float32"), "q2": ("sbuf", [128, 40], "float32"),
+    "ga": ("sbuf", [128, 640], "float32"), "bit": ("sbuf", [128, 640], "bfloat16"),
+    "sca": ("sbuf", [128, 320], "float32"), "scb": ("sbuf", [128, 320], "float32"),
+    "m1r": ("sbuf", [128, 320], "float32"), "fr": ("sbuf", [128, 320], "float32"), "lr": ("sbuf", [128, 320], "float32"),
+    "lw": ("sbuf", [128, 20], "uint16"), "ajr": ("sbuf", [128, 320], "float32"),
+    "kjr": ("sbuf", [128, 640], "float32"), "kjs": ("sbuf", [128, 640], "float32"),
+    "ddc": ("sbuf", [128, 20], "float32"), "kd": ("sbuf", [128, 20], "float32"), "kq": ("sbuf", [128, 20], "float32"),
+    "k1": ("sbuf", [128, 20], "float32"),
+    "tr": ("sbuf", [128, 320], "float32"), "gef": ("sbuf", [128, 20], "float32"), "vf": ("sbuf", [128, 20], "float32"),
+    "encf": ("sbuf", [128, 20], "float32"), "raw2": ("sbuf", [128, 320], "float32"),
+    "lohi": ("sbuf", [128, 20], "float32"), "rr": ("sbuf", [128, 20], "float32"),
+}
+for _k in (0, 1):
+    SCRATCH["sk%d" % _k] = ("sbuf", [128, 320], "float32")
+    SCRATCH["sum%d" % _k] = ("sbuf", [128, 320], "bfloat16")
+    SCRATCH["nx%d" % _k] = ("sbuf", [128, 320], "bfloat16")
+    SCRATCH["w%d" % _k] = ("sbuf", [128, 320], "bfloat16")
+    SCRATCH["mw%d" % _k] = ("sbuf", [128, 20], "uint16")
+    SCRATCH["xi%d" % _k] = ("sbuf", [128, 1280], "bfloat16")
+    SCRATCH["hvs%d" % _k] = ("sbuf", [128, 20], "uint16")
+    SCRATCH["hv%d" % _k] = ("sbuf", [128, 20], "uint16")
+    SCRATCH["lhr%d" % _k] = ("sbuf", [128, 320], "float32")
+for _n in range(4):
+    SCRATCH["enc%d" % _n] = ("sbuf", [128, 20], "uint16")
+    SCRATCH["pr%d" % _n] = ("sbuf", [128, 320], "float32")
+    SCRATCH["lhu%d" % _n] = ("sbuf", [128, 20], "uint16")
+for _r in (1, 2, 3):
+    SCRATCH["qh%d" % _r] = ("sbuf", [128, 320], CODE)
+    SCRATCH["sh%d" % _r] = ("sbuf", [128, 320], "uint8")
+    SCRATCH["lc%d" % _r] = ("sbuf", [128, 320], CODE)
+    SCRATCH["ls%d" % _r] = ("sbuf", [128, 320], "uint8")
+    SCRATCH["fw%d" % _r] = ("sbuf", [128, 20], "uint16")
+    SCRATCH["fp%d" % _r] = ("sbuf", [128, 20], "uint16")
+
+SEMAPHORES = ["qv_", "qs_", "qt_", "qg_", "dx", "dl", "du", "dw", "dv", "lsem", "oq", "oy", "ot"] + \
+    ["a%df" % r for r in (1, 2, 3)] + ["a%dc%d" % (r, c) for r in (1, 2, 3) for c in (0, 1)]
+
+
+def rank_program(g, core, T, topo):
+    rank = T.rank_of(core)
+    if rank is None:
+        return
+    Q = {"v": g.vector, "s": g.scalar, "t": g.tensor, "g": g, "y": g.sync}
+    SEM = {"v": "qv_", "s": "qs_", "t": "qt_", "g": "qg_"}
+    cnt = {}
+    known = {q: {} for q in Q}
+    snap = {}
+    wrote, read = {}, {}
+
+    def need(q, sem, val):
+        if known[q].get(sem, 0) >= val:
+            return
+        Q[q].wait_ge(T.sem[sem], val)
+        known[q][sem] = val
+        for k, w in snap.get((sem, val), {}).items():
+            if known[q].get(k, 0) < w:
+                known[q][k] = w
+
+    def order(q, rd, wr):
+        deps = {}
+        for t in rd:
+            for k, w in wrote.get(t, {}).items():
+                deps[k] = max(deps.get(k, 0), w)
+        for t in wr:
+            for d in (wrote.get(t, {}), read.get(t, {})):
+                for k, w in d.items():
+                    deps[k] = max(deps.get(k, 0), w)
+        for k, w in deps.items():
+            need(q, k, w)
+
+    def done(sem, val, rd, wr):
+        for t in rd:
+            d = read.setdefault(t, {})
+            d[sem] = max(d.get(sem, 0), val)
+        for t in wr:
+            wrote[t] = {sem: val}
+            read[t] = {}
+
+    def op(q, rd, wr, f):
+        order(q, rd, wr)
+        sem = SEM[q]
+        f().then_inc(T.sem[sem], 1)
+        cnt[sem] = cnt.get(sem, 0) + 1
+        snap[(sem, cnt[sem])] = dict(known[q])
+        done(sem, cnt[sem], rd, wr)
+
+    def dma(q, sem, out, in_, rd=(), wr=(), total=16):
+        order(q, rd, wr)
+        Q[q].dma_start(out, in_).then_inc(T.sem[sem], 16)
+        cnt[sem] = total
+        done(sem, total, rd, wr)
+
+    V, S, P = g.vector, g.scalar, g.tensor
+
+    def bank(k, n):
+        return T.ps[:, 512 * k:512 * k + n]
+
+    def lst(name, a=0, b=20):
+        return T[name][:, a:b]
+
+    def pick(name, off, a=0, n=C):
+        return T[name][:, a:a + n].indirect(off)
+
+    dma("s", "dl", T.hlt[:, 0:20], T.hl[:], wr=["hlt"], total=32)
+    dma("y", "dl", T.hlt[:, 20:40], T.tl[:], total=32)
+    dma("y", "dx", T.xi0[:], T.x[:], wr=["xi0.%d" % b for b in range(4)])
+    dma("s", "du", T.ut[:], T.u[:], wr=["ut"])
+    dma("y", "dw", T.qw[:].bitcast(dt.uint8), T.wc[:], wr=["qw"], total=32)
+    dma("y", "dw", T.sw[:], T.ws[:], total=32)
+    dma("y", "dv", T.vt[:], T.v[:], wr=["vt"])
+
+    op("g", [], ["pmi"], lambda: g.iota(T.pmi[:], [[0, 2]], 0, 1))
+    op("g", [], ["him"], lambda: g.iota(T.him[:], [[1, 320]], 128, -1))
+    op("g", [], ["cio"], lambda: g.iota(T.cio[:], [[1, 320]], 0, 0, allow_small_or_imprecise_dtypes=True))
+    op("g", [], ["uoi"], lambda: g.iota(T.uoi[:], [[1, 2], [16, 8]], 0, 0))
+    op("g", [], ["alt"], lambda: g.iota(T.alt[:], [[0, 160], [1, 2]], 0, 0, allow_small_or_imprecise_dtypes=True))
+    op("g", [], ["dec"], lambda: g.iota(T.dec[:], [[1, 2], [2, 160]], 0, 0, allow_small_or_imprecise_dtypes=True))
+    op("v", [], ["one"], lambda: V.memset(T.one[:], 1.0))
+    for b in range(4):
+        op("g", ["one"], ["et%d" % b], lambda: g.affine_select(T.et[:, 512 * b:512 * b + 512], T.one[:], [[-1, 512]], A.is_equal, 0.0, b, 4))
+    op("v", ["pmi"], ["pma"], lambda: V.tensor_scalar(T.pma[:], T.pmi[:], 15, None, A.bitwise_and))
+    op("v", ["him"], ["hia"], lambda: V.tensor_scalar(T.hia[:], T.him[:], 15, None, A.bitwise_and))
+    op("v", ["pma"], ["sub"], lambda: V.tensor_scalar(T["sub"][:], T.pma[:, 0:1], -512.0, 7680.0, A.mult, A.add))
+    op("v", ["hia"], ["mk"], lambda: V.tensor_scalar(T.mk[:], T.hia[:], 0.0, -16896.0, A.is_equal, A.mult))
+    op("v", ["pma"], ["cp"], lambda: V.tensor_scalar(T.cp[:], T.pma[:, 0:1], -2.0, 30.0, A.mult, A.add))
+    op("v", ["pma"], ["cp2"], lambda: V.tensor_scalar(T.cp2[:], T.pma[:, 0:1], -4.0, 61.0, A.mult, A.add))
+    op("s", ["mk"], ["hold"], lambda: S.activation(T.hold[:], T.mk[:], AF.Copy, bias=512.0))
+    op("s", ["mk"], ["holdb"], lambda: S.activation(T.holdb[:], T.mk[:], AF.Copy, bias=2.0, scale=0.00390625))
+
+    nsc = [0]
+
+    def wrap_scan(row, rtok):
+        nsc[0] += 1
+        b = ("sca", "scb")[nsc[0] % 2]
+        op("v", [rtok, "hold"], [b], lambda: V.tensor_tensor_scan(T[b][:], T.hold[:], row, 0.0, A.add, A.max))
+        return b
+
+    def wrap_out(b, out, otok):
+        op("v", [b, "sub"], [otok], lambda: V.tensor_scalar(out, T[b][:, 15:C:16], T["sub"][:], None, A.subtract))
+
+    def wrap(row, rtok, out, otok):
+        wrap_out(wrap_scan(row, rtok), out, otok)
+
+    def spread(name, off, otok, win="cio"):
+        op("s", [win, otok], [name], lambda: S.activation(T[name][:], pick(win, off), AF.Copy))
+
+    def spread_er(n):
+        op("s", ["cio", "enc%d" % n], ["er%d" % n], lambda: S.activation(T.er[:, C * n:C * n + C], pick("cio", lst("enc%d" % n)), AF.Copy))
+
+    def scatter(n):
+        op("v", ["enc%d" % n, "cio"], ["pr%d" % n], lambda: V.tensor_copy(T["pr%d" % n][:, 0:C].indirect(lst("enc%d" % n)), T.cio[:]))
+
+    def vertices(n):
+        b = wrap_scan(T["pr%d" % n][:], "pr%d" % n)
+
+        def rest():
+            op("v", [b], ["lo"], lambda: V.tensor_tensor(T.lohi[:, 0:10], T[b][:, 15:HC:16], T[b][:, HC + 15:C:16], A.min))
+            op("v", [b], ["hi"], lambda: V.tensor_tensor(T.lohi[:, 10:20], T[b][:, 15:HC:16], T[b][:, HC + 15:C:16], A.max))
+            op("v", ["lo", "hi", "sub"], ["lhu%d" % n], lambda: V.tensor_scalar(T["lhu%d" % n][:], T.lohi[:], T["sub"][:], None, A.subtract))
+        return rest
+
+    def places(n, src, stok):
+        m = n % 2
+        op("v", [stok], ["hv%d" % m], lambda: V.tensor_copy(T["hv%d" % m][:], src))
+        op("v", [stok], ["hvs%d" % m], lambda: V.tensor_scalar(T["hvs%d" % m][:], src, 2.0, 1.0, A.mult, A.add))
+
+    def rows(n):
+        spread("lhr%d" % (n % 2), lst("lhu%d" % n), "lhu%d" % n)
+
+    def role_pick(n):
+        m = n % 2
+        op("s", ["lhr%d" % m, "hv%d" % m], ["ajr"], lambda: S.activation(T.ajr[:], pick("lhr%d" % m, lst("hv%d" % m), 0, HC), AF.Copy))
+
+    def role(n):
+        m = n % 2
+        b = wrap_scan(T.ajr[:], "ajr")
+        op("v", [b, "ciw"], ["rr"], lambda: V.tensor_tensor(T.rr[:], T[b][:, 15:C:16], T.ciw[:, 15:C:16], A.not_equal))
+        op("v", ["rr"], ["g2%d" % m], lambda: V.tensor_scalar(T.g2[:, 20 * m:20 * m + 20], T.rr[:], 2.0, -1.0, A.mult, A.add))
+        op("v", ["rr", "cp", "cp2"], ["q2%d" % m], lambda: V.tensor_scalar(
+            T.q2[:, 20 * m:20 * m + 20], T.rr[:], T.cp2[:], T.cp[:], A.mult, A.subtract))
+
+    def cand_pick(n):
+        i, o = (n - 1) % 2, n % 2
+        for h in (0, 1):
+            op("s", ["lhr%d" % o, "hv%d" % i], ["kjr%d" % h], lambda: S.activation(
+                T.kjr[:, C * h:C * h + C], pick("lhr%d" % o, lst("hv%d" % i), HC * h, HC), AF.Copy))
+
+    def cand_scan(n):
+        for h in (0, 1):
+            op("v", ["kjr%d" % h, "hold"], ["kjs%d" % h], lambda: V.tensor_tensor_scan(
+                T.kjs[:, C * h:C * h + C], T.hold[:], T.kjr[:, C * h:C * h + C], 0.0, A.add, A.max))
+
+    def cand(n):
+        i = (n - 1) % 2
+        a, b = T.kjs[:, 15:C:16], T.kjs[:, C + 15:2 * C:16]
+        op("v", ["kjs0", "kjs1"], ["ddc"], lambda: V.tensor_tensor(T.ddc[:], b, a, A.subtract))
+        op("v", ["ddc", "q2%d" % i], ["kq"], lambda: V.tensor_tensor(T.kq[:], T.ddc[:], T.q2[:, 20 * i:20 * i + 20], A.mult))
+        op("v", ["ddc", "g2%d" % i], ["kd"], lambda: V.tensor_tensor(T.kd[:], T.ddc[:], T.g2[:, 20 * i:20 * i + 20], A.mult))
+        op("v", ["kjs1", "kq"], ["k1"], lambda: V.tensor_tensor(T.k1[:], b, T.kq[:], A.subtract))
+
+    op("v", ["hlt"], ["hb"], lambda: V.tensor_scalar(T.hb[:], T.hlt[:], 1, None, A.bitwise_and))
+    op("v", ["hlt"], ["hv"], lambda: V.tensor_scalar(T.hv[:], T.hlt[:], 1, None, A.arith_shift_right))
+    op("v", ["hb"], ["hb2"], lambda: V.tensor_scalar(T.hb2[:], T.hb[:], 160, None, A.mult))
+    op("v", ["hb2", "hv"], ["enci"], lambda: V.tensor_tensor(T.enci[:], T.hb2[:], T.hv[:], A.add))
+    for n in range(2):
+        op("v", ["enci"], ["enc%d" % n], lambda: V.tensor_copy(T["enc%d" % n][:], T.enci[:, 20 * n:20 * n + 20]))
+    scatter(0)
+    op("v", ["ut"], ["qu"], lambda: V.quantize_mx(T.qu[:], T.su[:], T.ut[:]))
+    op("v", ["uoi"], ["uof"], lambda: V.tensor_copy(T.uof[:], T.uoi[:]))
+    op("v", ["xi0.%d" % b for b in range(4)], ["qx"], lambda: V.quantize_mx(T.qx[:], T.sx[:], T.xi0[:]))
+    op("v", ["qu", "uof"], ["qu2"], lambda: V.tensor_copy(T.qu2[:].bitcast(dt.uint32), T.qu[:].bitcast(dt.uint32).indirect(T.uof[:])))
+    op("s", ["qu", "uof"], ["su2"], lambda: S.activation(T.su2[:], T.su[:].indirect(T.uof[:]), AF.Copy))
+    for b in range(4):
+        op("s", ["xi0.%d" % b], ["xp%d" % b], lambda: S.activation(T.xp[:, C * b:C * b + C], T.xi0[:, b:1280:4], AF.Copy))
+    vertices(0)()
+    rows(0)
+    spread_er(0)
+    spread_er(1)
+    scatter(1)
+    places(0, T.hv[:, 0:20], "hv")
+    role_pick(0)
+    vertices(1)()
+    rows(1)
+    cand_pick(1)
+
+    for r in (1, 2, 3):
+        last = r == 3
+        peer = T.cores[rank ^ STEP[r - 1]]
+        rid, pid = topo.addr(peer)[0], topo.addr(peer)[1]
+        mask = topo.mask(core, peer)
+        neng = len(topo.engines(core, peer))
+        xo, xn = "xi%d" % ((r - 1) % 2), "xi%d" % (r % 2)
+        ai, ao = "lhu%d" % (r - 1), "lhu%d" % r
+
+        for k in (1, 0):
+            op("t", ["qx", "qu2", "su2"], ["bk%d" % k], lambda: P.matmul_mx(
+                bank(k, C), T.qu2[:, 128 * k:128 * k + 128], T.su2[:, 128 * k:128 * k + 128], T.qx[:], T.sx[:], True, True))
+        for k in (1, 0):
+            op("v", [], ["bk%d" % k, "sk%d" % k], lambda: V.tensor_copy(T["sk%d" % k][:], bank(k, C)))
+        if r == 1:
+            op("v", ["cio", "hold"], ["ciw"], lambda: V.tensor_tensor_scan(T.ciw[:], T.hold[:], T.cio[:], 0.0, A.add, A.max))
+            role(0)
+            cand_scan(1)
+            cand(1)
+        for k in (1, 0):
+            sk, ga, bt = "sk%d" % k, "ga%d" % k, "bit%d" % k
+            for i, w in ((0, ai), (1, ao)):
+                op("s", [sk, w], [ga + ".%d" % i], lambda: S.activation(
+                    T.ga[:, C * k + HC * i:C * k + HC * i + HC], pick(sk, lst(w, 0, 10)), AF.Copy))
+            for i, w in ((0, ai), (1, ao)):
+                op("v", [sk, w, ga + ".%d" % i], [bt + ".%d" % i], lambda: V.tensor_tensor(
+                    T.bit[:, C * k + i:C * k + C:2], pick(sk, lst(w, 10, 20)), T.ga[:, C * k + HC * i:C * k + HC * i + HC], A.is_gt))
+            op("v", [bt + ".0", bt + ".1", "alt"], ["sum%d" % k], lambda: V.tensor_tensor_scan(
+                T["sum%d" % k][:], T.alt[:], T.bit[:, C * k:C * k + C], 0.0, A.mult, A.add))
+        hvs = "hvs%d" % ((r - 1) % 2)
+        for k in (1, 0):
+            op("s", ["sum%d" % k, hvs], ["nx%d" % k], lambda: S.activation(T["nx%d" % k][:], pick("sum%d" % k, lst(hvs)), AF.Square, bias=-1.0))
+
+        def yadd(b):
+            op("v", ["xp%d" % b, "%s.%d" % (xo, b), "mw1"], ["y%d" % b], lambda: V.tensor_tensor(
+                T.y32[:, C * b:C * b + C], pick("xp", lst("mw1"), C * b), T[xo][:, b:1280:4], A.add))
+
+        def move(k, i):
+            if i == 0:
+                op("v", ["nx%d" % k, "holdb"], ["w%d" % k], lambda: V.tensor_tensor_scan(T["w%d" % k][:], T.holdb[:], T["nx%d" % k][:], 0.0, A.add, A.max))
+            if i == 1:
+                op("v", ["w%d" % k, "kd"], ["mt%d" % k], lambda: V.tensor_tensor(T.mt[:, 20 * k:20 * k + 20], T["w%d" % k][:, 15:C:16], T.kd[:], A.mult))
+            if i == 2:
+                op("v", ["mt%d" % k, "k1"], ["mf%d" % k], lambda: V.tensor_tensor(T.mf[:, 20 * k:20 * k + 20], T.mt[:, 20 * k:20 * k + 20], T.k1[:], A.add))
+            if i == 3:
+                op("v", ["mf%d" % k, "sub"], ["mw%d" % k], lambda: V.tensor_scalar(
+                    T["mw%d" % k][:], T.mf[:, 20 * k:20 * k + 20], T["sub"][:], None, A.subtract))
+
+        fw, fp = "fw%d" % r, "fp%d" % r
+        for k, i in ((1, 0), (1, 1), (1, 2), (0, 0), (1, 3), (0, 1), (0, 2), (0, 3)):
+            move(k, i)
+        for b in (0, 1, 2):
+            yadd(b)
+        spread("m1r", lst("mw1"), "mw1")
+        op("s", ["m1r", "mw0"], ["fr"], lambda: S.activation(T.fr[:], pick("m1r", lst("mw0")), AF.Copy))
+        wrap(T.fr[:], "fr", T[fw][:], fw)
+        order("g", [fw], [])
+        g.remote_dma(T[fp][:], T[fw][:], T.sem["a%df" % r], T.sem.lsem, pid, rid, mask)
+        cnt["lsem"] = cnt.get("lsem", 0) + neng
+        yadd(3)
+
+        for b in range(3):
+            op("s", ["y%d" % b, "mw0"], ["z%d" % b], lambda: S.activation(T.zt[:, b:1280:4], pick("y32", lst("mw0"), C * b), AF.Copy, scale=0.5))
+        op("v", ["y3", "mw0"], ["z3"], lambda: V.tensor_scalar(T.zt[:, 3:640:4], pick("y32", lst("mw0", 0, 10), 3 * C), 0.5, None, A.mult))
+        op("s", ["y3", "mw0"], ["z4"], lambda: S.activation(T.zt[:, 643:1280:4], pick("y32", lst("mw0", 10, 20), 3 * C), AF.Copy, scale=0.5))
+        for c in (0, 1):
+            op("v", ["z0", "z1", "z2", "z%d" % (3 + c)], ["qz%d" % c], lambda: V.quantize_mx(
+                T.qz[:, HC * c:HC * c + HC], T.sz[:, HC * c:HC * c + HC], T.zt[:, 640 * c:640 * c + 640]))
+            for b in range(4):
+                op("t", ["qz%d" % c, "qw"], ["bk%d" % (4 * c + b)], lambda: P.matmul_mx(
+                    bank(4 * c + b, HC), T.qw[:, 128 * b:128 * b + 128], T.sw[:, 128 * b:128 * b + 128],
+                    T.qz[:, HC * c:HC * c + HC], T.sz[:, HC * c:HC * c + HC], True, True))
+        qh, sh, lc, ls = "qh%d" % r, "sh%d" % r, "lc%d" % r, "ls%d" % r
+        for c in (0, 1):
+            for b in range(4):
+                out = T.ht[:, 640 * c + b:640 * c + 640:4]
+                if b % 2 == 0:
+                    op("v", [], ["bk%d" % (4 * c + b), "h%d%d" % (c, b)], lambda: V.tensor_scalar(out, bank(4 * c + b, HC), 0.03125, None, A.mult))
+                else:
+                    op("s", [], ["bk%d" % (4 * c + b), "h%d%d" % (c, b)], lambda: S.activation(out, bank(4 * c + b, HC), AF.Copy, scale=0.03125))
+            op("v", ["h%d%d" % (c, b) for b in range(4)], [qh + str(c)], lambda: V.quantize_mx(
+                T[qh][:, HC * c:HC * c + HC], T[sh][:, HC * c:HC * c + HC], T.ht[:, 640 * c:640 * c + 640]))
+            order("g", [qh + str(c)], [])
+            for out, in_ in ((T[lc][:, HC * c:HC * c + HC].bitcast(dt.uint8), T[qh][:, HC * c:HC * c + HC].bitcast(dt.uint8)),
+                             (T[ls][:, HC * c:HC * c + HC], T[sh][:, HC * c:HC * c + HC])):
+                g.remote_dma(out, in_, T.sem["a%dc%d" % (r, c)], T.sem.lsem, pid, rid, mask)
+                cnt["lsem"] += neng
+        for sem, n in [("a%df" % r, neng), ("a%dc0" % r, 2 * neng), ("a%dc1" % r, 2 * neng)]:
+            cnt[sem] = n
+        wrote[fp] = {"a%df" % r: neng}
+        for c in (0, 1):
+            wrote["ld%d%d" % (r, c)] = {"a%dc%d" % (r, c): 2 * neng}
+
+        n = r + 1
+        if r == 1:
+            places(1, T.hv[:, 20:40], "hv")
+        elif r == 2:
+            op("v", ["enc2"], ["encf"], lambda: V.tensor_copy(T.encf[:], T.enc2[:]))
+            op("v", ["enc2"], ["gef"], lambda: V.tensor_scalar(T.gef[:], T.enc2[:], 160.0, -160.0, A.is_ge, A.mult))
+            op("v", ["encf", "gef"], ["vf"], lambda: V.tensor_tensor(T.vf[:], T.encf[:], T.gef[:], A.add))
+            places(2, T.vf[:], "vf")
+        else:
+            op("v", ["vt"], ["qv"], lambda: V.quantize_mx(T.qv[:], T.sv[:], T.vt[:]))
+            spread("raw2", lst("enc2"), "enc2", "dec")
+        if not last:
+            op("s", ["er%d" % (r - 1), fp], ["tr"], lambda: S.activation(T.tr[:], pick("er", lst(fp), C * (r - 1)), AF.Copy))
+            wrap(T.tr[:], "tr", T["enc%d" % n][:], "enc%d" % n)
+            scatter(n)
+        op("s", ["fr", fp], ["lr"], lambda: S.activation(T.lr[:], pick("fr", lst(fp)), AF.Copy))
+        if not last:
+            role_pick(r)
+            fin = vertices(n)
+            bl = wrap_scan(T.lr[:], "lr")
+            fin()
+            wrap_out(bl, T.lw[:], "lw")
+            rows(n)
+            cand_pick(n)
+            if r == 1:
+                for b in range(4):
+                    op("v", ["et%d" % b], ["qe%d" % b], lambda: V.quantize_mx(
+                        T.qe[:, 128 * b:128 * b + 128], T.se[:, 128 * b:128 * b + 128], T.et[:, 512 * b:512 * b + 512]))
+            role(r)
+            cand_scan(n)
+            cand(n)
+        else:
+            wrap(T.lr[:], "lr", T.lw[:], "lw")
+            op("s", ["raw2", fp], ["tpr"], lambda: S.activation(T.tpr[:], pick("raw2", lst(fp)), AF.Copy))
+            dma("y", "ot", T.tp[:], T.tpr[0:128:16, :], rd=["tpr"])
+
+        for c in (0, 1):
+            for b in range(4):
+                op("t", ["ld%d%d" % (r, c), "qe%d" % b], ["bk%d" % (4 * c + b)], lambda: P.matmul_mx(
+                    bank(4 * c + b, HC), T.qe[:, 128 * b:128 * b + 128], T.se[:, 128 * b:128 * b + 128],
+                    T[lc][:, HC * c:HC * c + HC], T[ls][:, HC * c:HC * c + HC], True, True))
+            for b in range(4):
+                out = T.dd[:, C * b + HC * c:C * b + HC * c + HC]
+                if b == 0 or c == 1 and b == 2:
+                    op("v", [], ["bk%d" % (4 * c + b), "d%d%d" % (c, b)], lambda: V.tensor_copy(out, bank(4 * c + b, HC)))
+                else:
+                    op("s", [], ["bk%d" % (4 * c + b), "d%d%d" % (c, b)], lambda: S.activation(out, bank(4 * c + b, HC), AF.Copy))
+        for b in range(4):
+            op("v", ["d0%d" % b, "d1%d" % b, "lw", "%s.%d" % (xo, b)], ["%s.%d" % (xn, b)], lambda: V.tensor_tensor(
+                T[xn][:, b:1280:4], pick("dd", lst("lw"), C * b), T[xo][:, b:1280:4], A.add))
+        toks = ["%s.%d" % (xn, b) for b in range(4)]
+        if not last:
+            op("v", toks, ["qx"], lambda: V.quantize_mx(T.qx[:], T.sx[:], T[xn][:]))
+            for b in range(4):
+                op("s", [toks[b]], ["xp%d" % b], lambda: S.activation(T.xp[:, C * b:C * b + C], T[xn][:, b:1280:4], AF.Copy))
+        else:
+            op("v", toks, ["qo"], lambda: V.quantize_mx(T.qo[:], T.so[:], T[xn][:]))
+
+    dma("y", "oq", T.oc[:], T.qo[:].bitcast(dt.uint8), rd=["qo"], total=80)
+    for k in range(4):
+        dma("s" if k % 2 else "y", "oq", T.osc[4 * k:4 * k + 4, :], T.so[32 * k:32 * k + 4, :], rd=["qo"], total=80)
+    for c in (0, 1):
+        op("t", ["qo", "qv"], ["bk%d" % c], lambda: P.matmul_mx(
+            bank(c, HC), T.qv[:], T.sv[:], T.qo[:, HC * c:HC * c + HC], T.so[:, HC * c:HC * c + HC], True, True))
+    op("v", [], ["bk0", "yo0"], lambda: V.tensor_copy(T.yo[:, 0:HC], bank(0, HC)))
+    op("s", [], ["bk1", "yo1"], lambda: S.activation(T.yo[:, HC:C], bank(1, HC), AF.Copy))
+    for c, q in ((0, "y"), (1, "s")):
+        dma(q, "oy", T.y[:, HC * c:HC * c + HC], T.yo[:, HC * c:HC * c + HC], rd=["yo%d" % c], total=32)
+    for sem in sorted(cnt):
+        need("g", sem, cnt[sem])

@@ -12,7 +12,8 @@ SCRATCH = {
     "him": ("sbuf", [128, 320], "int32"), "hia": ("sbuf", [128, 320], "int32"), "mk": ("sbuf", [128, 320], "float32"),
     "hold": ("sbuf", [128, 320], "float32"), "holdb": ("sbuf", [128, 320], "bfloat16"), "alt": ("sbuf", [128, 320], "bfloat16"),
     "pmi": ("sbuf", [128, 2], "int32"), "pma": ("sbuf", [128, 2], "int32"), "sub": ("sbuf", [128, 1], "float32"),
-    "cp": ("sbuf", [128, 1], "float32"), "cp2": ("sbuf", [128, 1], "float32"), "ciw": ("sbuf", [128, 320], "float32"),
+    "cp": ("sbuf", [128, 1], "float32"), "cp2": ("sbuf", [128, 1], "float32"), "cs": ("sbuf", [128, 1], "float32"),
+    "c16": ("sbuf", [128, 20], "float32"), "ciw": ("sbuf", [128, 20], "float32"),
     "uoi": ("sbuf", [128, 16], "int32"), "uof": ("sbuf", [128, 16], "uint16"),
     "one": ("sbuf", [128, 512], "bfloat16"), "et": ("sbuf", [128, 2048], "bfloat16"),
     "qe": ("sbuf", [128, 512], CODE), "se": ("sbuf", [128, 512], "uint8"),
@@ -30,7 +31,8 @@ SCRATCH = {
     "qo": ("sbuf", [128, 320], CODE), "so": ("sbuf", [128, 320], "uint8"),
     "yo": ("sbuf", [128, 320], "float32"), "tpr": ("sbuf", [128, 320], "float32"),
     "ps": ("psum", [128, 4096], "float32"),
-    "mt": ("sbuf", [128, 40], "float32"), "mf": ("sbuf", [128, 40], "float32"), "er": ("sbuf", [128, 640], "float32"),
+    "fi": ("sbuf", [128, 320], "float32"),
+    "mt": ("sbuf", [128, 40], "float32"), "mf": ("sbuf", [128, 40], "float32"),
     "g2": ("sbuf", [128, 40], "float32"), "q2": ("sbuf", [128, 40], "float32"),
     "ga": ("sbuf", [128, 640], "float32"), "bit": ("sbuf", [128, 640], "bfloat16"),
     "sca": ("sbuf", [128, 320], "float32"), "scb": ("sbuf", [128, 320], "float32"),
@@ -38,9 +40,9 @@ SCRATCH = {
     "lw": ("sbuf", [128, 20], "uint16"), "ajr": ("sbuf", [128, 320], "float32"),
     "kjr": ("sbuf", [128, 640], "float32"), "kjs": ("sbuf", [128, 640], "float32"),
     "ddc": ("sbuf", [128, 20], "float32"), "kd": ("sbuf", [128, 20], "float32"), "kq": ("sbuf", [128, 20], "float32"),
-    "k1": ("sbuf", [128, 20], "float32"),
-    "tr": ("sbuf", [128, 320], "float32"), "gef": ("sbuf", [128, 20], "float32"), "vf": ("sbuf", [128, 20], "float32"),
-    "encf": ("sbuf", [128, 20], "float32"), "raw2": ("sbuf", [128, 320], "float32"),
+    "k1": ("sbuf", [128, 20], "float32"), "kx": ("sbuf", [128, 20], "float32"), "kc": ("sbuf", [128, 20], "float32"),
+    "tr": ("sbuf", [128, 320], "float32"), "cvm": ("sbuf", [128, 320], "float32"), "hvr": ("sbuf", [128, 320], "float32"),
+    "raw0": ("sbuf", [128, 320], "float32"), "raw2": ("sbuf", [128, 320], "float32"),
     "lohi": ("sbuf", [128, 20], "float32"), "rr": ("sbuf", [128, 20], "float32"),
 }
 for _k in (0, 1):
@@ -54,7 +56,8 @@ for _k in (0, 1):
     SCRATCH["hv%d" % _k] = ("sbuf", [128, 20], "uint16")
     SCRATCH["lhr%d" % _k] = ("sbuf", [128, 320], "float32")
 for _n in range(4):
-    SCRATCH["enc%d" % _n] = ("sbuf", [128, 20], "uint16")
+    if _n < 2:
+        SCRATCH["enc%d" % _n] = ("sbuf", [128, 20], "uint16")
     SCRATCH["pr%d" % _n] = ("sbuf", [128, 320], "float32")
     SCRATCH["lhu%d" % _n] = ("sbuf", [128, 20], "uint16")
 for _r in (1, 2, 3):
@@ -144,9 +147,11 @@ def rank_program(g, core, T, topo):
 
     op("g", [], ["pmi"], lambda: g.iota(T.pmi[:], [[0, 2]], 0, 1))
     op("g", [], ["him"], lambda: g.iota(T.him[:], [[1, 320]], 128, -1))
+    op("g", [], ["c16"], lambda: g.iota(T.c16[:], [[16, 20]], 0, 0, allow_small_or_imprecise_dtypes=True))
     op("g", [], ["cio"], lambda: g.iota(T.cio[:], [[1, 320]], 0, 0, allow_small_or_imprecise_dtypes=True))
     op("g", [], ["uoi"], lambda: g.iota(T.uoi[:], [[1, 2], [16, 8]], 0, 0))
     op("g", [], ["alt"], lambda: g.iota(T.alt[:], [[0, 160], [1, 2]], 0, 0, allow_small_or_imprecise_dtypes=True))
+    op("g", [], ["cvm"], lambda: g.iota(T.cvm[:], [[0, 2], [1, 160]], 0, 0, allow_small_or_imprecise_dtypes=True))
     op("g", [], ["dec"], lambda: g.iota(T.dec[:], [[1, 2], [2, 160]], 0, 0, allow_small_or_imprecise_dtypes=True))
     op("v", [], ["one"], lambda: V.memset(T.one[:], 1.0))
     for b in range(4):
@@ -154,9 +159,11 @@ def rank_program(g, core, T, topo):
     op("v", ["pmi"], ["pma"], lambda: V.tensor_scalar(T.pma[:], T.pmi[:], 15, None, A.bitwise_and))
     op("v", ["him"], ["hia"], lambda: V.tensor_scalar(T.hia[:], T.him[:], 15, None, A.bitwise_and))
     op("v", ["pma"], ["sub"], lambda: V.tensor_scalar(T["sub"][:], T.pma[:, 0:1], -512.0, 7680.0, A.mult, A.add))
+    op("v", ["pma"], ["cs"], lambda: V.tensor_scalar(T.cs[:], T.pma[:, 0:1], -511.0, 7680.0, A.mult, A.add))
     op("v", ["hia"], ["mk"], lambda: V.tensor_scalar(T.mk[:], T.hia[:], 0.0, -16896.0, A.is_equal, A.mult))
     op("v", ["pma"], ["cp"], lambda: V.tensor_scalar(T.cp[:], T.pma[:, 0:1], -2.0, 30.0, A.mult, A.add))
     op("v", ["pma"], ["cp2"], lambda: V.tensor_scalar(T.cp2[:], T.pma[:, 0:1], -4.0, 61.0, A.mult, A.add))
+    op("v", ["c16", "cs"], ["ciw"], lambda: V.tensor_scalar(T.ciw[:], T.c16[:], T.cs[:], None, A.add))
     op("s", ["mk"], ["hold"], lambda: S.activation(T.hold[:], T.mk[:], AF.Copy, bias=512.0))
     op("s", ["mk"], ["holdb"], lambda: S.activation(T.holdb[:], T.mk[:], AF.Copy, bias=2.0, scale=0.00390625))
 
@@ -176,9 +183,6 @@ def rank_program(g, core, T, topo):
 
     def spread(name, off, otok, win="cio"):
         op("s", [win, otok], [name], lambda: S.activation(T[name][:], pick(win, off), AF.Copy))
-
-    def spread_er(n):
-        op("s", ["cio", "enc%d" % n], ["er%d" % n], lambda: S.activation(T.er[:, C * n:C * n + C], pick("cio", lst("enc%d" % n)), AF.Copy))
 
     def scatter(n):
         op("v", ["enc%d" % n, "cio"], ["pr%d" % n], lambda: V.tensor_copy(T["pr%d" % n][:, 0:C].indirect(lst("enc%d" % n)), T.cio[:]))
@@ -207,16 +211,16 @@ def rank_program(g, core, T, topo):
     def role(n):
         m = n % 2
         b = wrap_scan(T.ajr[:], "ajr")
-        op("v", [b, "ciw"], ["rr"], lambda: V.tensor_tensor(T.rr[:], T[b][:, 15:C:16], T.ciw[:, 15:C:16], A.not_equal))
+        op("v", [b, "ciw"], ["rr"], lambda: V.tensor_tensor(T.rr[:], T[b][:, 15:C:16], T.ciw[:], A.not_equal))
         op("v", ["rr"], ["g2%d" % m], lambda: V.tensor_scalar(T.g2[:, 20 * m:20 * m + 20], T.rr[:], 2.0, -1.0, A.mult, A.add))
         op("v", ["rr", "cp", "cp2"], ["q2%d" % m], lambda: V.tensor_scalar(
             T.q2[:, 20 * m:20 * m + 20], T.rr[:], T.cp2[:], T.cp[:], A.mult, A.subtract))
 
     def cand_pick(n):
-        i, o = (n - 1) % 2, n % 2
+        i = (n - 1) % 2
         for h in (0, 1):
-            op("s", ["lhr%d" % o, "hv%d" % i], ["kjr%d" % h], lambda: S.activation(
-                T.kjr[:, C * h:C * h + C], pick("lhr%d" % o, lst("hv%d" % i), HC * h, HC), AF.Copy))
+            op("s", ["pr%d" % n, "hv%d" % i], ["kjr%d" % h], lambda: S.activation(
+                T.kjr[:, C * h:C * h + C], pick("pr%d" % n, lst("hv%d" % i), HC * h, HC), AF.Copy))
 
     def cand_scan(n):
         for h in (0, 1):
@@ -226,35 +230,48 @@ def rank_program(g, core, T, topo):
     def cand(n):
         i = (n - 1) % 2
         a, b = T.kjs[:, 15:C:16], T.kjs[:, C + 15:2 * C:16]
-        op("v", ["kjs0", "kjs1"], ["ddc"], lambda: V.tensor_tensor(T.ddc[:], b, a, A.subtract))
+        op("v", ["kjs0", "kjs1"], ["kx"], lambda: V.tensor_tensor(T.kx[:], a, b, A.max))
+        op("v", ["kjs0", "kjs1"], ["kc"], lambda: V.tensor_tensor(T.kc[:], a, b, A.min))
+        op("v", ["kx", "kc"], ["ddc"], lambda: V.tensor_tensor(T.ddc[:], T.kx[:], T.kc[:], A.subtract))
+
+    def cand_b(n):
+        i = (n - 1) % 2
         op("v", ["ddc", "q2%d" % i], ["kq"], lambda: V.tensor_tensor(T.kq[:], T.ddc[:], T.q2[:, 20 * i:20 * i + 20], A.mult))
         op("v", ["ddc", "g2%d" % i], ["kd"], lambda: V.tensor_tensor(T.kd[:], T.ddc[:], T.g2[:, 20 * i:20 * i + 20], A.mult))
-        op("v", ["kjs1", "kq"], ["k1"], lambda: V.tensor_tensor(T.k1[:], b, T.kq[:], A.subtract))
+        op("v", ["kx", "kq"], ["k1"], lambda: V.tensor_tensor(T.k1[:], T.kx[:], T.kq[:], A.subtract))
 
     op("v", ["hlt"], ["hb"], lambda: V.tensor_scalar(T.hb[:], T.hlt[:], 1, None, A.bitwise_and))
     op("v", ["hlt"], ["hv"], lambda: V.tensor_scalar(T.hv[:], T.hlt[:], 1, None, A.arith_shift_right))
     op("v", ["hb"], ["hb2"], lambda: V.tensor_scalar(T.hb2[:], T.hb[:], 160, None, A.mult))
     op("v", ["hb2", "hv"], ["enci"], lambda: V.tensor_tensor(T.enci[:], T.hb2[:], T.hv[:], A.add))
-    for n in range(2):
+    for n in (1, 0):
         op("v", ["enci"], ["enc%d" % n], lambda: V.tensor_copy(T["enc%d" % n][:], T.enci[:, 20 * n:20 * n + 20]))
-    scatter(0)
+    scatter(1)
+    fin = vertices(1)
+    places(0, T.hv[:, 0:20], "hv")
+    fin()
     op("v", ["ut"], ["qu"], lambda: V.quantize_mx(T.qu[:], T.su[:], T.ut[:]))
     op("v", ["uoi"], ["uof"], lambda: V.tensor_copy(T.uof[:], T.uoi[:]))
-    op("v", ["xi0.%d" % b for b in range(4)], ["qx"], lambda: V.quantize_mx(T.qx[:], T.sx[:], T.xi0[:]))
+
+    def quant_x(name):
+        for c in (0, 1):
+            op("v", ["%s.%d" % (name, b) for b in range(4)], ["qx%d" % c], lambda: V.quantize_mx(
+                T.qx[:, HC * c:HC * c + HC], T.sx[:, HC * c:HC * c + HC], T[name][:, 640 * c:640 * c + 640]))
+
+    def plane(b, name):
+        op("s", ["%s.%d" % (name, b)], ["xp%d" % b], lambda: S.activation(T.xp[:, C * b:C * b + C], T[name][:, b:1280:4], AF.Copy))
+
+    quant_x("xi0")
+    for b in range(3):
+        plane(b, "xi0")
     op("v", ["qu", "uof"], ["qu2"], lambda: V.tensor_copy(T.qu2[:].bitcast(dt.uint32), T.qu[:].bitcast(dt.uint32).indirect(T.uof[:])))
     op("s", ["qu", "uof"], ["su2"], lambda: S.activation(T.su2[:], T.su[:].indirect(T.uof[:]), AF.Copy))
-    for b in range(4):
-        op("s", ["xi0.%d" % b], ["xp%d" % b], lambda: S.activation(T.xp[:, C * b:C * b + C], T.xi0[:, b:1280:4], AF.Copy))
+    cand_pick(1)
+    rows(1)
+    scatter(0)
     vertices(0)()
     rows(0)
-    spread_er(0)
-    spread_er(1)
-    scatter(1)
-    places(0, T.hv[:, 0:20], "hv")
     role_pick(0)
-    vertices(1)()
-    rows(1)
-    cand_pick(1)
 
     for r in (1, 2, 3):
         last = r == 3
@@ -266,28 +283,41 @@ def rank_program(g, core, T, topo):
         ai, ao = "lhu%d" % (r - 1), "lhu%d" % r
 
         for k in (1, 0):
-            op("t", ["qx", "qu2", "su2"], ["bk%d" % k], lambda: P.matmul_mx(
-                bank(k, C), T.qu2[:, 128 * k:128 * k + 128], T.su2[:, 128 * k:128 * k + 128], T.qx[:], T.sx[:], True, True))
+            for c in (0, 1):
+                op("t", ["qx%d" % c, "qu2", "su2"], ["bk%d" % (2 * k + c)], lambda: P.matmul_mx(
+                    bank(2 * k + c, HC), T.qu2[:, 128 * k:128 * k + 128], T.su2[:, 128 * k:128 * k + 128],
+                    T.qx[:, HC * c:HC * c + HC], T.sx[:, HC * c:HC * c + HC], True, True))
         for k in (1, 0):
-            op("v", [], ["bk%d" % k, "sk%d" % k], lambda: V.tensor_copy(T["sk%d" % k][:], bank(k, C)))
+            for c in (0, 1):
+                out, in_, tok = T["sk%d" % k][:, HC * c:HC * c + HC], bank(2 * k + c, HC), ["bk%d" % (2 * k + c), "sk%d.%d" % (k, c)]
+                if r > 1 and (k, c) == (1, 0):
+                    op("s", [], tok, lambda: S.activation(out, in_, AF.Copy))
+                else:
+                    op("v", [], tok, lambda: V.tensor_copy(out, in_))
         if r == 1:
-            op("v", ["cio", "hold"], ["ciw"], lambda: V.tensor_tensor_scan(T.ciw[:], T.hold[:], T.cio[:], 0.0, A.add, A.max))
-            role(0)
             cand_scan(1)
-            cand(1)
+        cand(r)
         for k in (1, 0):
             sk, ga, bt = "sk%d" % k, "ga%d" % k, "bit%d" % k
             for i, w in ((0, ai), (1, ao)):
-                op("s", [sk, w], [ga + ".%d" % i], lambda: S.activation(
+                op("s", [sk + ".0", sk + ".1", w], [ga + ".%d" % i], lambda: S.activation(
                     T.ga[:, C * k + HC * i:C * k + HC * i + HC], pick(sk, lst(w, 0, 10)), AF.Copy))
             for i, w in ((0, ai), (1, ao)):
-                op("v", [sk, w, ga + ".%d" % i], [bt + ".%d" % i], lambda: V.tensor_tensor(
+                op("v", [sk + ".0", sk + ".1", w, ga + ".%d" % i], [bt + ".%d" % i], lambda: V.tensor_tensor(
                     T.bit[:, C * k + i:C * k + C:2], pick(sk, lst(w, 10, 20)), T.ga[:, C * k + HC * i:C * k + HC * i + HC], A.is_gt))
             op("v", [bt + ".0", bt + ".1", "alt"], ["sum%d" % k], lambda: V.tensor_tensor_scan(
                 T["sum%d" % k][:], T.alt[:], T.bit[:, C * k:C * k + C], 0.0, A.mult, A.add))
+            if k == 1 and r == 1:
+                role(0)
+        if r == 1:
+            places(1, T.hv[:, 20:40], "hv")
+        cand_b(r)
         hvs = "hvs%d" % ((r - 1) % 2)
         for k in (1, 0):
             op("s", ["sum%d" % k, hvs], ["nx%d" % k], lambda: S.activation(T["nx%d" % k][:], pick("sum%d" % k, lst(hvs)), AF.Square, bias=-1.0))
+
+        if r == 1:
+            plane(3, "xi0")
 
         def yadd(b):
             op("v", ["xp%d" % b, "%s.%d" % (xo, b), "mw1"], ["y%d" % b], lambda: V.tensor_tensor(
@@ -310,11 +340,25 @@ def rank_program(g, core, T, topo):
         for b in (0, 1, 2):
             yadd(b)
         spread("m1r", lst("mw1"), "mw1")
-        op("s", ["m1r", "mw0"], ["fr"], lambda: S.activation(T.fr[:], pick("m1r", lst("mw0")), AF.Copy))
+
+        def pick_f():
+            op("s", ["m1r", "mw0"], ["fr"], lambda: S.activation(T.fr[:], pick("m1r", lst("mw0")), AF.Copy))
+
+        def send_f():
+            order("g", [fw], [])
+            g.remote_dma(T[fp][:], T[fw][:], T.sem["a%df" % r], T.sem.lsem, pid, rid, mask)
+            cnt["lsem"] = cnt.get("lsem", 0) + neng
+
+        def heads():
+            if r == 1:
+                role(1)
+            elif r == 2:
+                wrap(T.tr[:], "tr", T.hv0[:], "hv0")
+                op("v", ["hv0"], ["hvs0"], lambda: V.tensor_scalar(T.hvs0[:], T.hv0[:], 2.0, 1.0, A.mult, A.add))
+
+        pick_f()
         wrap(T.fr[:], "fr", T[fw][:], fw)
-        order("g", [fw], [])
-        g.remote_dma(T[fp][:], T[fw][:], T.sem["a%df" % r], T.sem.lsem, pid, rid, mask)
-        cnt["lsem"] = cnt.get("lsem", 0) + neng
+        send_f()
         yadd(3)
 
         for b in range(3):
@@ -329,8 +373,12 @@ def rank_program(g, core, T, topo):
                     bank(4 * c + b, HC), T.qw[:, 128 * b:128 * b + 128], T.sw[:, 128 * b:128 * b + 128],
                     T.qz[:, HC * c:HC * c + HC], T.sz[:, HC * c:HC * c + HC], True, True))
         qh, sh, lc, ls = "qh%d" % r, "sh%d" % r, "lc%d" % r, "ls%d" % r
+        if r == 1:
+            role_pick(1)
         for c in (0, 1):
             for b in range(4):
+                if (c, b) == (0, 2):
+                    heads()
                 out = T.ht[:, 640 * c + b:640 * c + 640:4]
                 if b % 2 == 0:
                     op("v", [], ["bk%d" % (4 * c + b), "h%d%d" % (c, b)], lambda: V.tensor_scalar(out, bank(4 * c + b, HC), 0.03125, None, A.mult))
@@ -350,41 +398,37 @@ def rank_program(g, core, T, topo):
             wrote["ld%d%d" % (r, c)] = {"a%dc%d" % (r, c): 2 * neng}
 
         n = r + 1
-        if r == 1:
-            places(1, T.hv[:, 20:40], "hv")
-        elif r == 2:
-            op("v", ["enc2"], ["encf"], lambda: V.tensor_copy(T.encf[:], T.enc2[:]))
-            op("v", ["enc2"], ["gef"], lambda: V.tensor_scalar(T.gef[:], T.enc2[:], 160.0, -160.0, A.is_ge, A.mult))
-            op("v", ["encf", "gef"], ["vf"], lambda: V.tensor_tensor(T.vf[:], T.encf[:], T.gef[:], A.add))
-            places(2, T.vf[:], "vf")
-        else:
-            op("v", ["vt"], ["qv"], lambda: V.quantize_mx(T.qv[:], T.sv[:], T.vt[:]))
-            spread("raw2", lst("enc2"), "enc2", "dec")
         if not last:
-            op("s", ["er%d" % (r - 1), fp], ["tr"], lambda: S.activation(T.tr[:], pick("er", lst(fp), C * (r - 1)), AF.Copy))
-            wrap(T.tr[:], "tr", T["enc%d" % n][:], "enc%d" % n)
-            scatter(n)
-        op("s", ["fr", fp], ["lr"], lambda: S.activation(T.lr[:], pick("fr", lst(fp)), AF.Copy))
-        if not last:
-            role_pick(r)
-            fin = vertices(n)
-            bl = wrap_scan(T.lr[:], "lr")
-            fin()
-            wrap_out(bl, T.lw[:], "lw")
-            rows(n)
-            cand_pick(n)
+            op("v", [fp, "cio"], ["fi"], lambda: V.tensor_copy(T.fi[:, 0:C].indirect(lst(fp)), T.cio[:]))
             if r == 1:
                 for b in range(4):
                     op("v", ["et%d" % b], ["qe%d" % b], lambda: V.quantize_mx(
                         T.qe[:, 128 * b:128 * b + 128], T.se[:, 128 * b:128 * b + 128], T.et[:, 512 * b:512 * b + 512]))
-            role(r)
-            cand_scan(n)
-            cand(n)
         else:
+            op("v", ["vt"], ["qv"], lambda: V.quantize_mx(T.qv[:], T.sv[:], T.vt[:]))
+        op("s", ["fr", fp], ["lr"], lambda: S.activation(T.lr[:], pick("fr", lst(fp)), AF.Copy))
+        if not last:
+            if r == 1:
+                op("s", ["cvm", "enc0"], ["hvr"], lambda: S.activation(T.hvr[:], pick("cvm", lst("enc0")), AF.Copy))
+            else:
+                rows(2)
+                role_pick(2)
+            op("s", ["fi", "lhu%d" % (r - 1)], ["pr%d" % n], lambda: S.activation(T["pr%d" % n][:], pick("fi", lst("lhu%d" % (r - 1))), AF.Copy))
+            wrap(T.lr[:], "lr", T.lw[:], "lw")
+            vertices(n)()
+            cand_pick(n)
+            if r == 2:
+                role(2)
+            cand_scan(n)
+        else:
+            spread("raw0", lst("enc0"), "enc0", "dec")
+            spread("raw2", lst("fp1"), "fp1", "raw0")
             wrap(T.lr[:], "lr", T.lw[:], "lw")
             op("s", ["raw2", fp], ["tpr"], lambda: S.activation(T.tpr[:], pick("raw2", lst(fp)), AF.Copy))
             dma("y", "ot", T.tp[:], T.tpr[0:128:16, :], rd=["tpr"])
 
+        if r == 1:
+            op("s", ["hvr", fp], ["tr"], lambda: S.activation(T.tr[:], pick("hvr", lst(fp)), AF.Copy))
         for c in (0, 1):
             for b in range(4):
                 op("t", ["ld%d%d" % (r, c), "qe%d" % b], ["bk%d" % (4 * c + b)], lambda: P.matmul_mx(
@@ -392,7 +436,7 @@ def rank_program(g, core, T, topo):
                     T[lc][:, HC * c:HC * c + HC], T[ls][:, HC * c:HC * c + HC], True, True))
             for b in range(4):
                 out = T.dd[:, C * b + HC * c:C * b + HC * c + HC]
-                if b == 0 or c == 1 and b == 2:
+                if b == 0 and c == 1:
                     op("v", [], ["bk%d" % (4 * c + b), "d%d%d" % (c, b)], lambda: V.tensor_copy(out, bank(4 * c + b, HC)))
                 else:
                     op("s", [], ["bk%d" % (4 * c + b), "d%d%d" % (c, b)], lambda: S.activation(out, bank(4 * c + b, HC), AF.Copy))
@@ -401,21 +445,23 @@ def rank_program(g, core, T, topo):
                 T[xn][:, b:1280:4], pick("dd", lst("lw"), C * b), T[xo][:, b:1280:4], A.add))
         toks = ["%s.%d" % (xn, b) for b in range(4)]
         if not last:
-            op("v", toks, ["qx"], lambda: V.quantize_mx(T.qx[:], T.sx[:], T[xn][:]))
+            quant_x(xn)
             for b in range(4):
-                op("s", [toks[b]], ["xp%d" % b], lambda: S.activation(T.xp[:, C * b:C * b + C], T[xn][:, b:1280:4], AF.Copy))
+                plane(b, xn)
         else:
-            op("v", toks, ["qo"], lambda: V.quantize_mx(T.qo[:], T.so[:], T[xn][:]))
+            for c in (0, 1):
+                op("v", toks, ["qo%d" % c], lambda: V.quantize_mx(
+                    T.qo[:, HC * c:HC * c + HC], T.so[:, HC * c:HC * c + HC], T[xn][:, 640 * c:640 * c + 640]))
 
-    dma("y", "oq", T.oc[:], T.qo[:].bitcast(dt.uint8), rd=["qo"], total=80)
+    dma("y", "oq", T.oc[:], T.qo[:].bitcast(dt.uint8), rd=["qo0", "qo1"], total=80)
     for k in range(4):
-        dma("s" if k % 2 else "y", "oq", T.osc[4 * k:4 * k + 4, :], T.so[32 * k:32 * k + 4, :], rd=["qo"], total=80)
+        dma("y", "oq", T.osc[4 * k:4 * k + 4, :], T.so[32 * k:32 * k + 4, :], rd=["qo0", "qo1"], total=80)
     for c in (0, 1):
-        op("t", ["qo", "qv"], ["bk%d" % c], lambda: P.matmul_mx(
+        op("t", ["qo%d" % c, "qv"], ["bk%d" % c], lambda: P.matmul_mx(
             bank(c, HC), T.qv[:], T.sv[:], T.qo[:, HC * c:HC * c + HC], T.so[:, HC * c:HC * c + HC], True, True))
     op("v", [], ["bk0", "yo0"], lambda: V.tensor_copy(T.yo[:, 0:HC], bank(0, HC)))
     op("s", [], ["bk1", "yo1"], lambda: S.activation(T.yo[:, HC:C], bank(1, HC), AF.Copy))
-    for c, q in ((0, "y"), (1, "s")):
-        dma(q, "oy", T.y[:, HC * c:HC * c + HC], T.yo[:, HC * c:HC * c + HC], rd=["yo%d" % c], total=32)
+    for c in (0, 1):
+        dma("s", "oy", T.y[:, HC * c:HC * c + HC], T.yo[:, HC * c:HC * c + HC], rd=["yo%d" % c], total=32)
     for sem in sorted(cnt):
         need("g", sem, cnt[sem])

from concourse.mybir import dt, AluOpType, ActivationFunctionType

A = AluOpType
AF = ActivationFunctionType
C = 320
HC = 160
STEP = [1, 2, 4]
CODE = "float8_e4m3fn_x4"

SCRATCH = {
    "cio": ("sbuf", [128, 320], "float32"), "dec": ("sbuf", [128, 320], "float32"),
    "him": ("sbuf", [128, 320], "int32"), "hia": ("sbuf", [128, 320], "int32"), "mk": ("sbuf", [128, 320], "float32"),
    "hold": ("sbuf", [128, 320], "float32"), "holdb": ("sbuf", [128, 320], "bfloat16"), "alt": ("sbuf", [128, 320], "bfloat16"),
    "pmi": ("sbuf", [128, 2], "int32"), "pma": ("sbuf", [128, 2], "int32"), "sub": ("sbuf", [128, 1], "float32"),
    "cp": ("sbuf", [128, 1], "float32"), "cp2": ("sbuf", [128, 1], "float32"), "cs": ("sbuf", [128, 1], "float32"),
    "c16": ("sbuf", [128, 20], "float32"), "ciw": ("sbuf", [128, 20], "float32"),
    "uoi": ("sbuf", [128, 16], "int32"), "uof": ("sbuf", [128, 16], "uint16"),
    "one": ("sbuf", [128, 512], "bfloat16"), "et": ("sbuf", [128, 2048], "bfloat16"),
    "qe": ("sbuf", [128, 512], CODE), "se": ("sbuf", [128, 512], "uint8"),
    "ut": ("sbuf", [128, 512], "bfloat16"), "vt": ("sbuf", [128, 512], "bfloat16"),
    "qu": ("sbuf", [128, 128], CODE), "su": ("sbuf", [128, 128], "uint8"),
    "qu2": ("sbuf", [128, 256], CODE), "su2": ("sbuf", [128, 256], "uint8"),
    "qv": ("sbuf", [128, 128], CODE), "sv": ("sbuf", [128, 128], "uint8"),
    "qw": ("sbuf", [128, 512], CODE), "sw": ("sbuf", [128, 512], "uint8"),
    "hlt": ("sbuf", [128, 40], "int32"), "hb": ("sbuf", [128, 40], "int32"), "hv": ("sbuf", [128, 40], "int32"),
    "hb2": ("sbuf", [128, 40], "int32"), "enci": ("sbuf", [128, 40], "int32"),
    "xp": ("sbuf", [128, 1280], "bfloat16"), "y32": ("sbuf", [128, 1280], "float32"), "zt": ("sbuf", [128, 1280], "bfloat16"),
    "ht": ("sbuf", [128, 1280], "bfloat16"), "dd": ("sbuf", [128, 1280], "bfloat16"),
    "qz": ("sbuf", [128, 320], CODE), "sz": ("sbuf", [128, 320], "uint8"),
    "qx": ("sbuf", [128, 320], CODE), "sx": ("sbuf", [128, 320], "uint8"),
    "qo": ("sbuf", [128, 320], CODE), "so": ("sbuf", [128, 320], "uint8"),
    "yo": ("sbuf", [128, 320], "float32"), "tpr": ("sbuf", [128, 320], "float32"),
    "ps": ("psum", [128, 4096], "float32"),
    "fi": ("sbuf", [128, 320], "float32"),
    "mt": ("sbuf", [128, 40], "float32"), "mf": ("sbuf", [128, 40], "float32"),
    "g2": ("sbuf", [128, 40], "float32"), "q2": ("sbuf", [128, 40], "float32"),
    "ga": ("sbuf", [128, 640], "float32"), "bit": ("sbuf", [128, 640], "bfloat16"),
    "sca": ("sbuf", [128, 320], "float32"), "scb": ("sbuf", [128, 320], "float32"),
    "m1r": ("sbuf", [128, 320], "float32"), "fr": ("sbuf", [128, 320], "float32"), "lr": ("sbuf", [128, 320], "float32"),
    "lw": ("sbuf", [128, 20], "uint16"), "ajr": ("sbuf", [128, 320], "float32"),
    "kjr": ("sbuf", [128, 640], "float32"), "kjs": ("sbuf", [128, 640], "float32"),
    "ddc": ("sbuf", [128, 20], "float32"), "kd": ("sbuf", [128, 20], "float32"), "kq": ("sbuf", [128, 20], "float32"),
    "k1": ("sbuf", [128, 20], "float32"), "kx": ("sbuf", [128, 20], "float32"), "kc": ("sbuf", [128, 20], "float32"),
    "tr": ("sbuf", [128, 320], "float32"), "cvm": ("sbuf", [128, 320], "float32"), "hvr": ("sbuf", [128, 320], "float32"),
    "raw0": ("sbuf", [128, 320], "float32"), "raw2": ("sbuf", [128, 320], "float32"),
    "lohi": ("sbuf", [128, 20], "float32"), "rr": ("sbuf", [128, 20], "float32"),
}
for _k in (0, 1):
    SCRATCH["sk%d" % _k] = ("sbuf", [128, 320], "float32")
    SCRATCH["sum%d" % _k] = ("sbuf", [128, 320], "bfloat16")
    SCRATCH["nx%d" % _k] = ("sbuf", [128, 320], "bfloat16")
    SCRATCH["w%d" % _k] = ("sbuf", [128, 320], "bfloat16")
    SCRATCH["mw%d" % _k] = ("sbuf", [128, 20], "uint16")
    SCRATCH["xi%d" % _k] = ("sbuf", [128, 1280], "bfloat16")
    SCRATCH["hvs%d" % _k] = ("sbuf", [128, 20], "uint16")
    SCRATCH["hv%d" % _k] = ("sbuf", [128, 20], "uint16")
    SCRATCH["lhr%d" % _k] = ("sbuf", [128, 320], "float32")
for _n in range(4):
    if _n < 2:
        SCRATCH["enc%d" % _n] = ("sbuf", [128, 20], "uint16")
    SCRATCH["pr%d" % _n] = ("sbuf", [128, 320], "float32")
    SCRATCH["lhu%d" % _n] = ("sbuf", [128, 20], "uint16")
for _r in (1, 2, 3):
    SCRATCH["qh%d" % _r] = ("sbuf", [128, 320], CODE)
    SCRATCH["sh%d" % _r] = ("sbuf", [128, 320], "uint8")
    SCRATCH["lc%d" % _r] = ("sbuf", [128, 320], CODE)
    SCRATCH["ls%d" % _r] = ("sbuf", [128, 320], "uint8")
    SCRATCH["fw%d" % _r] = ("sbuf", [128, 20], "uint16")
    SCRATCH["fp%d" % _r] = ("sbuf", [128, 20], "uint16")

SEMAPHORES = ["qv_", "qs_", "qt_", "qg_", "dx", "dl", "du", "dw", "dv", "lsem", "oq", "oy", "ot"] + \
    ["a%df" % r for r in (1, 2, 3)] + ["a%dc%d" % (r, c) for r in (1, 2, 3) for c in (0, 1)]


def rank_program(g, core, T, topo):
    rank = T.rank_of(core)
    if rank is None:
        return
    Q = {"v": g.vector, "s": g.scalar, "t": g.tensor, "g": g, "y": g.sync}
    SEM = {"v": "qv_", "s": "qs_", "t": "qt_", "g": "qg_"}
    cnt = {}
    known = {q: {} for q in Q}
    snap = {}
    wrote, read = {}, {}

    def need(q, sem, val):
        if known[q].get(sem, 0) >= val:
            return
        Q[q].wait_ge(T.sem[sem], val)
        known[q][sem] = val
        for k, w in snap.get((sem, val), {}).items():
            if known[q].get(k, 0) < w:
                known[q][k] = w

    def order(q, rd, wr):
        deps = {}
        for t in rd:
            for k, w in wrote.get(t, {}).items():
                deps[k] = max(deps.get(k, 0), w)
        for t in wr:
            for d in (wrote.get(t, {}), read.get(t, {})):
                for k, w in d.items():
                    deps[k] = max(deps.get(k, 0), w)
        for k, w in deps.items():
            need(q, k, w)

    def done(sem, val, rd, wr):
        for t in rd:
            d = read.setdefault(t, {})
            d[sem] = max(d.get(sem, 0), val)
        for t in wr:
            wrote[t] = {sem: val}
            read[t] = {}

    def op(q, rd, wr, f):
        order(q, rd, wr)
        sem = SEM[q]
        f().then_inc(T.sem[sem], 1)
        cnt[sem] = cnt.get(sem, 0) + 1
        snap[(sem, cnt[sem])] = dict(known[q])
        done(sem, cnt[sem], rd, wr)

    def dma(q, sem, out, in_, rd=(), wr=(), total=16):
        order(q, rd, wr)
        Q[q].dma_start(out, in_).then_inc(T.sem[sem], 16)
        cnt[sem] = total
        done(sem, total, rd, wr)

    V, S, P = g.vector, g.scalar, g.tensor

    def bank(k, n):
        return T.ps[:, 512 * k:512 * k + n]

    def lst(name, a=0, b=20):
        return T[name][:, a:b]

    def pick(name, off, a=0, n=C):
        return T[name][:, a:a + n].indirect(off)

    dma("s", "dl", T.hlt[:, 0:20], T.hl[:], wr=["hlt"], total=32)
    dma("y", "dl", T.hlt[:, 20:40], T.tl[:], total=32)
    dma("y", "dx", T.xi0[:], T.x[:], wr=["xi0.%d" % b for b in range(4)])
    dma("s", "du", T.ut[:], T.u[:], wr=["ut"])
    dma("y", "dw", T.qw[:].bitcast(dt.uint8), T.wc[:], wr=["qw"], total=32)
    dma("y", "dw", T.sw[:], T.ws[:], total=32)
    dma("y", "dv", T.vt[:], T.v[:], wr=["vt"])

    op("g", [], ["pmi"], lambda: g.iota(T.pmi[:], [[0, 2]], 0, 1))
    op("g", [], ["him"], lambda: g.iota(T.him[:], [[1, 320]], 128, -1))
    op("g", [], ["c16"], lambda: g.iota(T.c16[:], [[16, 20]], 0, 0, allow_small_or_imprecise_dtypes=True))
    op("g", [], ["cio"], lambda: g.iota(T.cio[:], [[1, 320]], 0, 0, allow_small_or_imprecise_dtypes=True))
    op("g", [], ["uoi"], lambda: g.iota(T.uoi[:], [[1, 2], [16, 8]], 0, 0))
    op("g", [], ["alt"], lambda: g.iota(T.alt[:], [[0, 160], [1, 2]], 0, 0, allow_small_or_imprecise_dtypes=True))
    op("g", [], ["cvm"], lambda: g.iota(T.cvm[:], [[0, 2], [1, 160]], 0, 0, allow_small_or_imprecise_dtypes=True))
    op("g", [], ["dec"], lambda: g.iota(T.dec[:], [[1, 2], [2, 160]], 0, 0, allow_small_or_imprecise_dtypes=True))
    op("v", [], ["one"], lambda: V.memset(T.one[:], 1.0))
    for b in range(4):
        op("g", ["one"], ["et%d" % b], lambda: g.affine_select(T.et[:, 512 * b:512 * b + 512], T.one[:], [[-1, 512]], A.is_equal, 0.0, b, 4))
    op("v", ["pmi"], ["pma"], lambda: V.tensor_scalar(T.pma[:], T.pmi[:], 15, None, A.bitwise_and))
    op("v", ["him"], ["hia"], lambda: V.tensor_scalar(T.hia[:], T.him[:], 15, None, A.bitwise_and))
    op("v", ["pma"], ["sub"], lambda: V.tensor_scalar(T["sub"][:], T.pma[:, 0:1], -512.0, 7680.0, A.mult, A.add))
    op("v", ["pma"], ["cs"], lambda: V.tensor_scalar(T.cs[:], T.pma[:, 0:1], -511.0, 7680.0, A.mult, A.add))
    op("v", ["hia"], ["mk"], lambda: V.tensor_scalar(T.mk[:], T.hia[:], 0.0, -16896.0, A.is_equal, A.mult))
    op("v", ["pma"], ["cp"], lambda: V.tensor_scalar(T.cp[:], T.pma[:, 0:1], -2.0, 30.0, A.mult, A.add))
    op("v", ["pma"], ["cp2"], lambda: V.tensor_scalar(T.cp2[:], T.pma[:, 0:1], -4.0, 61.0, A.mult, A.add))
    op("v", ["c16", "cs"], ["ciw"], lambda: V.tensor_scalar(T.ciw[:], T.c16[:], T.cs[:], None, A.add))
    op("s", ["mk"], ["hold"], lambda: S.activation(T.hold[:], T.mk[:], AF.Copy, bias=512.0))
    op("s", ["mk"], ["holdb"], lambda: S.activation(T.holdb[:], T.mk[:], AF.Copy, bias=2.0, scale=0.00390625))

    nsc = [0]

    def wrap_scan(row, rtok):
        nsc[0] += 1
        b = ("sca", "scb")[nsc[0] % 2]
        op("v", [rtok, "hold"], [b], lambda: V.tensor_tensor_scan(T[b][:], T.hold[:], row, 0.0, A.add, A.max))
        return b

    def wrap_out(b, out, otok):
        op("v", [b, "sub"], [otok], lambda: V.tensor_scalar(out, T[b][:, 15:C:16], T["sub"][:], None, A.subtract))

    def wrap(row, rtok, out, otok):
        wrap_out(wrap_scan(row, rtok), out, otok)

    def spread(name, off, otok, win="cio"):
        op("s", [win, otok], [name], lambda: S.activation(T[name][:], pick(win, off), AF.Copy))

    def scatter(n):
        op("v", ["enc%d" % n, "cio"], ["pr%d" % n], lambda: V.tensor_copy(T["pr%d" % n][:, 0:C].indirect(lst("enc%d" % n)), T.cio[:]))

    def vertices(n):
        b = wrap_scan(T["pr%d" % n][:], "pr%d" % n)

        def rest():
            op("v", [b], ["lo"], lambda: V.tensor_tensor(T.lohi[:, 0:10], T[b][:, 15:HC:16], T[b][:, HC + 15:C:16], A.min))
            op("v", [b], ["hi"], lambda: V.tensor_tensor(T.lohi[:, 10:20], T[b][:, 15:HC:16], T[b][:, HC + 15:C:16], A.max))
            op("v", ["lo", "hi", "sub"], ["lhu%d" % n], lambda: V.tensor_scalar(T["lhu%d" % n][:], T.lohi[:], T["sub"][:], None, A.subtract))
        return rest

    def places(n, src, stok):
        m = n % 2
        op("v", [stok], ["hv%d" % m], lambda: V.tensor_copy(T["hv%d" % m][:], src))
        op("v", [stok], ["hvs%d" % m], lambda: V.tensor_scalar(T["hvs%d" % m][:], src, 2.0, 1.0, A.mult, A.add))

    def rows(n):
        spread("lhr%d" % (n % 2), lst("lhu%d" % n), "lhu%d" % n)

    def role_pick(n):
        m = n % 2
        op("s", ["lhr%d" % m, "hv%d" % m], ["ajr"], lambda: S.activation(T.ajr[:], pick("lhr%d" % m, lst("hv%d" % m), 0, HC), AF.Copy))

    def role(n):
        m = n % 2
        b = wrap_scan(T.ajr[:], "ajr")
        op("v", [b, "ciw"], ["rr"], lambda: V.tensor_tensor(T.rr[:], T[b][:, 15:C:16], T.ciw[:], A.not_equal))
        op("v", ["rr"], ["g2%d" % m], lambda: V.tensor_scalar(T.g2[:, 20 * m:20 * m + 20], T.rr[:], 2.0, -1.0, A.mult, A.add))
        op("v", ["rr", "cp", "cp2"], ["q2%d" % m], lambda: V.tensor_scalar(
            T.q2[:, 20 * m:20 * m + 20], T.rr[:], T.cp2[:], T.cp[:], A.mult, A.subtract))

    def cand_pick(n):
        i = (n - 1) % 2
        for h in (0, 1):
            op("s", ["pr%d" % n, "hv%d" % i], ["kjr%d" % h], lambda: S.activation(
                T.kjr[:, C * h:C * h + C], pick("pr%d" % n, lst("hv%d" % i), HC * h, HC), AF.Copy))

    def cand_scan(n):
        for h in (0, 1):
            op("v", ["kjr%d" % h, "hold"], ["kjs%d" % h], lambda: V.tensor_tensor_scan(
                T.kjs[:, C * h:C * h + C], T.hold[:], T.kjr[:, C * h:C * h + C], 0.0, A.add, A.max))

    def cand(n):
        i = (n - 1) % 2
        a, b = T.kjs[:, 15:C:16], T.kjs[:, C + 15:2 * C:16]
        op("v", ["kjs0", "kjs1"], ["kx"], lambda: V.tensor_tensor(T.kx[:], a, b, A.max))
        op("v", ["kjs0", "kjs1"], ["kc"], lambda: V.tensor_tensor(T.kc[:], a, b, A.min))
        op("v", ["kx", "kc"], ["ddc"], lambda: V.tensor_tensor(T.ddc[:], T.kx[:], T.kc[:], A.subtract))

    def cand_b(n):
        i = (n - 1) % 2
        op("v", ["ddc", "q2%d" % i], ["kq"], lambda: V.tensor_tensor(T.kq[:], T.ddc[:], T.q2[:, 20 * i:20 * i + 20], A.mult))
        op("v", ["ddc", "g2%d" % i], ["kd"], lambda: V.tensor_tensor(T.kd[:], T.ddc[:], T.g2[:, 20 * i:20 * i + 20], A.mult))
        op("v", ["kx", "kq"], ["k1"], lambda: V.tensor_tensor(T.k1[:], T.kx[:], T.kq[:], A.subtract))

    op("v", ["hlt"], ["hb"], lambda: V.tensor_scalar(T.hb[:], T.hlt[:], 1, None, A.bitwise_and))
    op("v", ["hlt"], ["hv"], lambda: V.tensor_scalar(T.hv[:], T.hlt[:], 1, None, A.arith_shift_right))
    op("v", ["hb"], ["hb2"], lambda: V.tensor_scalar(T.hb2[:], T.hb[:], 160, None, A.mult))
    op("v", ["hb2", "hv"], ["enci"], lambda: V.tensor_tensor(T.enci[:], T.hb2[:], T.hv[:], A.add))
    for n in (1, 0):
        op("v", ["enci"], ["enc%d" % n], lambda: V.tensor_copy(T["enc%d" % n][:], T.enci[:, 20 * n:20 * n + 20]))
    scatter(1)
    fin = vertices(1)
    places(0, T.hv[:, 0:20], "hv")
    fin()
    op("v", ["ut"], ["qu"], lambda: V.quantize_mx(T.qu[:], T.su[:], T.ut[:]))
    op("v", ["uoi"], ["uof"], lambda: V.tensor_copy(T.uof[:], T.uoi[:]))

    def quant_x(name):
        for c in (0, 1):
            op("v", ["%s.%d" % (name, b) for b in range(4)], ["qx%d" % c], lambda: V.quantize_mx(
                T.qx[:, HC * c:HC * c + HC], T.sx[:, HC * c:HC * c + HC], T[name][:, 640 * c:640 * c + 640]))

    def plane(b, name):
        op("s", ["%s.%d" % (name, b)], ["xp%d" % b], lambda: S.activation(T.xp[:, C * b:C * b + C], T[name][:, b:1280:4], AF.Copy))

    quant_x("xi0")
    for b in range(3):
        plane(b, "xi0")
    op("v", ["qu", "uof"], ["qu2"], lambda: V.tensor_copy(T.qu2[:].bitcast(dt.uint32), T.qu[:].bitcast(dt.uint32).indirect(T.uof[:])))
    op("s", ["qu", "uof"], ["su2"], lambda: S.activation(T.su2[:], T.su[:].indirect(T.uof[:]), AF.Copy))
    cand_pick(1)
    rows(1)
    scatter(0)
    vertices(0)()
    rows(0)
    role_pick(0)

    for r in (1, 2, 3):
        last = r == 3
        peer = T.cores[rank ^ STEP[r - 1]]
        rid, pid = topo.addr(peer)[0], topo.addr(peer)[1]
        mask = topo.mask(core, peer)
        neng = len(topo.engines(core, peer))
        xo, xn = "xi%d" % ((r - 1) % 2), "xi%d" % (r % 2)
        ai, ao = "lhu%d" % (r - 1), "lhu%d" % r

        for k in (1, 0):
            for c in (0, 1):
                op("t", ["qx%d" % c, "qu2", "su2"], ["bk%d" % (2 * k + c)], lambda: P.matmul_mx(
                    bank(2 * k + c, HC), T.qu2[:, 128 * k:128 * k + 128], T.su2[:, 128 * k:128 * k + 128],
                    T.qx[:, HC * c:HC * c + HC], T.sx[:, HC * c:HC * c + HC], True, True))
        for k in (1, 0):
            for c in (0, 1):
                out, in_, tok = T["sk%d" % k][:, HC * c:HC * c + HC], bank(2 * k + c, HC), ["bk%d" % (2 * k + c), "sk%d.%d" % (k, c)]
                if r > 1 and (k, c) == (1, 0):
                    op("s", [], tok, lambda: S.activation(out, in_, AF.Copy))
                else:
                    op("v", [], tok, lambda: V.tensor_copy(out, in_))
        if r == 1:
            cand_scan(1)
        cand(r)
        for k in (1, 0):
            sk, ga, bt = "sk%d" % k, "ga%d" % k, "bit%d" % k
            for i, w in ((0, ai), (1, ao)):
                op("s", [sk + ".0", sk + ".1", w], [ga + ".%d" % i], lambda: S.activation(
                    T.ga[:, C * k + HC * i:C * k + HC * i + HC], pick(sk, lst(w, 0, 10)), AF.Copy))
            for i, w in ((0, ai), (1, ao)):
                op("v", [sk + ".0", sk + ".1", w, ga + ".%d" % i], [bt + ".%d" % i], lambda: V.tensor_tensor(
                    T.bit[:, C * k + i:C * k + C:2], pick(sk, lst(w, 10, 20)), T.ga[:, C * k + HC * i:C * k + HC * i + HC], A.is_gt))
            op("v", [bt + ".0", bt + ".1", "alt"], ["sum%d" % k], lambda: V.tensor_tensor_scan(
                T["sum%d" % k][:], T.alt[:], T.bit[:, C * k:C * k + C], 0.0, A.mult, A.add))
            if k == 1 and r == 1:
                role(0)
        if r == 1:
            places(1, T.hv[:, 20:40], "hv")
        cand_b(r)
        hvs = "hvs%d" % ((r - 1) % 2)
        for k in (1, 0):
            op("s", ["sum%d" % k, hvs], ["nx%d" % k], lambda: S.activation(T["nx%d" % k][:], pick("sum%d" % k, lst(hvs)), AF.Square, bias=-1.0))

        if r == 1:
            plane(3, "xi0")

        def yadd(b):
            op("v", ["xp%d" % b, "%s.%d" % (xo, b), "mw1"], ["y%d" % b], lambda: V.tensor_tensor(
                T.y32[:, C * b:C * b + C], pick("xp", lst("mw1"), C * b), T[xo][:, b:1280:4], A.add))

        def move(k, i):
            if i == 0:
                op("v", ["nx%d" % k, "holdb"], ["w%d" % k], lambda: V.tensor_tensor_scan(T["w%d" % k][:], T.holdb[:], T["nx%d" % k][:], 0.0, A.add, A.max))
            if i == 1:
                op("v", ["w%d" % k, "kd"], ["mt%d" % k], lambda: V.tensor_tensor(T.mt[:, 20 * k:20 * k + 20], T["w%d" % k][:, 15:C:16], T.kd[:], A.mult))
            if i == 2:
                op("v", ["mt%d" % k, "k1"], ["mf%d" % k], lambda: V.tensor_tensor(T.mf[:, 20 * k:20 * k + 20], T.mt[:, 20 * k:20 * k + 20], T.k1[:], A.add))
            if i == 3:
                op("v", ["mf%d" % k, "sub"], ["mw%d" % k], lambda: V.tensor_scalar(
                    T["mw%d" % k][:], T.mf[:, 20 * k:20 * k + 20], T["sub"][:], None, A.subtract))

        fw, fp = "fw%d" % r, "fp%d" % r
        for k, i in ((1, 0), (1, 1), (1, 2), (0, 0), (1, 3), (0, 1), (0, 2), (0, 3)):
            move(k, i)
        for b in (0, 1, 2):
            yadd(b)
        spread("m1r", lst("mw1"), "mw1")

        def pick_f():
            op("s", ["m1r", "mw0"], ["fr"], lambda: S.activation(T.fr[:], pick("m1r", lst("mw0")), AF.Copy))

        def send_f():
            order("g", [fw], [])
            g.remote_dma(T[fp][:], T[fw][:], T.sem["a%df" % r], T.sem.lsem, pid, rid, mask)
            cnt["lsem"] = cnt.get("lsem", 0) + neng

        def heads():
            if r == 1:
                role(1)
            elif r == 2:
                wrap(T.tr[:], "tr", T.hv0[:], "hv0")
                op("v", ["hv0"], ["hvs0"], lambda: V.tensor_scalar(T.hvs0[:], T.hv0[:], 2.0, 1.0, A.mult, A.add))

        pick_f()
        wrap(T.fr[:], "fr", T[fw][:], fw)
        send_f()
        yadd(3)

        for b in range(3):
            op("s", ["y%d" % b, "mw0"], ["z%d" % b], lambda: S.activation(T.zt[:, b:1280:4], pick("y32", lst("mw0"), C * b), AF.Copy, scale=0.5))
        op("v", ["y3", "mw0"], ["z3"], lambda: V.tensor_scalar(T.zt[:, 3:640:4], pick("y32", lst("mw0", 0, 10), 3 * C), 0.5, None, A.mult))
        op("s", ["y3", "mw0"], ["z4"], lambda: S.activation(T.zt[:, 643:1280:4], pick("y32", lst("mw0", 10, 20), 3 * C), AF.Copy, scale=0.5))
        for c in (0, 1):
            op("v", ["z0", "z1", "z2", "z%d" % (3 + c)], ["qz%d" % c], lambda: V.quantize_mx(
                T.qz[:, HC * c:HC * c + HC], T.sz[:, HC * c:HC * c + HC], T.zt[:, 640 * c:640 * c + 640]))
            for b in range(4):
                op("t", ["qz%d" % c, "qw"], ["bk%d" % (4 * c + b)], lambda: P.matmul_mx(
                    bank(4 * c + b, HC), T.qw[:, 128 * b:128 * b + 128], T.sw[:, 128 * b:128 * b + 128],
                    T.qz[:, HC * c:HC * c + HC], T.sz[:, HC * c:HC * c + HC], True, True))
        qh, sh, lc, ls = "qh%d" % r, "sh%d" % r, "lc%d" % r, "ls%d" % r
        if r == 1:
            role_pick(1)
        for c in (0, 1):
            for b in range(4):
                if (c, b) == (0, 2):
                    heads()
                out = T.ht[:, 640 * c + b:640 * c + 640:4]
                if b % 2 == 0:
                    op("v", [], ["bk%d" % (4 * c + b), "h%d%d" % (c, b)], lambda: V.tensor_scalar(out, bank(4 * c + b, HC), 0.03125, None, A.mult))
                else:
                    op("s", [], ["bk%d" % (4 * c + b), "h%d%d" % (c, b)], lambda: S.activation(out, bank(4 * c + b, HC), AF.Copy, scale=0.03125))
            op("v", ["h%d%d" % (c, b) for b in range(4)], [qh + str(c)], lambda: V.quantize_mx(
                T[qh][:, HC * c:HC * c + HC], T[sh][:, HC * c:HC * c + HC], T.ht[:, 640 * c:640 * c + 640]))
            order("g", [qh + str(c)], [])
            for out, in_ in ((T[lc][:, HC * c:HC * c + HC].bitcast(dt.uint8), T[qh][:, HC * c:HC * c + HC].bitcast(dt.uint8)),
                             (T[ls][:, HC * c:HC * c + HC], T[sh][:, HC * c:HC * c + HC])):
                g.remote_dma(out, in_, T.sem["a%dc%d" % (r, c)], T.sem.lsem, pid, rid, mask)
                cnt["lsem"] += neng
        for sem, n in [("a%df" % r, neng), ("a%dc0" % r, 2 * neng), ("a%dc1" % r, 2 * neng)]:
            cnt[sem] = n
        wrote[fp] = {"a%df" % r: neng}
        for c in (0, 1):
            wrote["ld%d%d" % (r, c)] = {"a%dc%d" % (r, c): 2 * neng}

        n = r + 1
        if not last:
            op("v", [fp, "cio"], ["fi"], lambda: V.tensor_copy(T.fi[:, 0:C].indirect(lst(fp)), T.cio[:]))
            if r == 1:
                for b in range(4):
                    op("v", ["et%d" % b], ["qe%d" % b], lambda: V.quantize_mx(
                        T.qe[:, 128 * b:128 * b + 128], T.se[:, 128 * b:128 * b + 128], T.et[:, 512 * b:512 * b + 512]))
        else:
            op("v", ["vt"], ["qv"], lambda: V.quantize_mx(T.qv[:], T.sv[:], T.vt[:]))
        op("s", ["fr", fp], ["lr"], lambda: S.activation(T.lr[:], pick("fr", lst(fp)), AF.Copy))
        if not last:
            if r == 1:
                op("s", ["cvm", "enc0"], ["hvr"], lambda: S.activation(T.hvr[:], pick("cvm", lst("enc0")), AF.Copy))
            else:
                rows(2)
                role_pick(2)
            op("s", ["fi", "lhu%d" % (r - 1)], ["pr%d" % n], lambda: S.activation(T["pr%d" % n][:], pick("fi", lst("lhu%d" % (r - 1))), AF.Copy))
            wrap(T.lr[:], "lr", T.lw[:], "lw")
            vertices(n)()
            cand_pick(n)
            if r == 2:
                role(2)
            cand_scan(n)
        else:
            spread("raw0", lst("enc0"), "enc0", "dec")
            spread("raw2", lst("fp1"), "fp1", "raw0")
            wrap(T.lr[:], "lr", T.lw[:], "lw")
            op("s", ["raw2", fp], ["tpr"], lambda: S.activation(T.tpr[:], pick("raw2", lst(fp)), AF.Copy))
            dma("y", "ot", T.tp[:], T.tpr[0:128:16, :], rd=["tpr"])

        if r == 1:
            op("s", ["hvr", fp], ["tr"], lambda: S.activation(T.tr[:], pick("hvr", lst(fp)), AF.Copy))
        for c in (0, 1):
            for b in range(4):
                op("t", ["ld%d%d" % (r, c), "qe%d" % b], ["bk%d" % (4 * c + b)], lambda: P.matmul_mx(
                    bank(4 * c + b, HC), T.qe[:, 128 * b:128 * b + 128], T.se[:, 128 * b:128 * b + 128],
                    T[lc][:, HC * c:HC * c + HC], T[ls][:, HC * c:HC * c + HC], True, True))
            for b in range(4):
                out = T.dd[:, C * b + HC * c:C * b + HC * c + HC]
                if b == 0 and c == 1:
                    op("v", [], ["bk%d" % (4 * c + b), "d%d%d" % (c, b)], lambda: V.tensor_copy(out, bank(4 * c + b, HC)))
                else:
                    op("s", [], ["bk%d" % (4 * c + b), "d%d%d" % (c, b)], lambda: S.activation(out, bank(4 * c + b, HC), AF.Copy))
        for b in range(4):
            op("v", ["d0%d" % b, "d1%d" % b, "lw", "%s.%d" % (xo, b)], ["%s.%d" % (xn, b)], lambda: V.tensor_tensor(
                T[xn][:, b:1280:4], pick("dd", lst("lw"), C * b), T[xo][:, b:1280:4], A.add))
        toks = ["%s.%d" % (xn, b) for b in range(4)]
        if not last:
            quant_x(xn)
            for b in range(4):
                plane(b, xn)
        else:
            for c in (0, 1):
                op("v", toks, ["qo%d" % c], lambda: V.quantize_mx(
                    T.qo[:, HC * c:HC * c + HC], T.so[:, HC * c:HC * c + HC], T[xn][:, 640 * c:640 * c + 640]))

    dma("y", "oq", T.oc[:], T.qo[:].bitcast(dt.uint8), rd=["qo0", "qo1"], total=80)
    for k in range(4):
        dma("y", "oq", T.osc[4 * k:4 * k + 4, :], T.so[32 * k:32 * k + 4, :], rd=["qo0", "qo1"], total=80)
    for c in (0, 1):
        op("t", ["qo%d" % c, "qv"], ["bk%d" % c], lambda: P.matmul_mx(
            bank(c, HC), T.qv[:], T.sv[:], T.qo[:, HC * c:HC * c + HC], T.so[:, HC * c:HC * c + HC], True, True))
    op("v", [], ["bk0", "yo0"], lambda: V.tensor_copy(T.yo[:, 0:HC], bank(0, HC)))
    op("s", [], ["bk1", "yo1"], lambda: S.activation(T.yo[:, HC:C], bank(1, HC), AF.Copy))
    for c in (0, 1):
        dma("s", "oy", T.y[:, HC * c:HC * c + HC], T.yo[:, HC * c:HC * c + HC], rd=["yo%d" % c], total=32)
    for sem in sorted(cnt):
        need("g", sem, cnt[sem])
